import numpy as np
import ml_dtypes


def mxq(x, axis, fmt="e4m3"):
    dtype, down = {"e4m3": (ml_dtypes.float8_e4m3fn, 7), "e5m2": (ml_dtypes.float8_e5m2, 14)}[fmt]
    v = np.moveaxis(np.asarray(x, np.float32).astype(ml_dtypes.bfloat16).astype(np.float64), axis, -1)
    blocks = v.reshape(v.shape[:-1] + (-1, 32))
    amax = np.abs(blocks).max(-1, keepdims=True)
    byte = np.maximum(np.where(amax > 0, np.frexp(amax)[1] - 1 + 127, 0) - down, 1)
    scale = np.exp2(byte - 127.0)
    codes = (blocks / scale).astype(np.float32).astype(dtype).astype(np.float64)
    return np.moveaxis((codes * scale).reshape(v.shape), -1, axis)


WIDE = False


def mx_kscale(k):
    if not WIDE:
        return np.ones(k)
    levels = np.array([10, -10, 5, -5, 0])
    if k % 512:
        return np.exp2(np.random.permutation(np.resize(levels, k // 32))).repeat(32)
    a = np.empty((k // 512, 16))
    for p in range(k // 512):
        a[p, :8] = np.random.permutation(np.resize(levels, 8))
        for g in range(8):
            far = levels[np.abs(levels - a[p, g]) >= 10]
            a[p, g + 8] = far[np.random.randint(len(far))]
    return np.exp2(a.ravel()).repeat(32)


def f64(x):
    return np.asarray(x).astype(np.float64)


def striped(idx):
    return np.tile(np.asarray(idx).reshape(-1, 16).T, (8, 1)).astype(np.uint16)


def unstriped(offs):
    return offs[:16].T.reshape(-1).astype(np.int64)


E2M1 = np.array([0.0, 0.5, 1.0, 1.5, 2.0, 3.0, 4.0, 6.0, -0.0, -0.5, -1.0, -1.5, -2.0, -3.0, -4.0, -6.0])


def pack_weight(w, fmt):
    k, n = w.shape
    w = f64(np.asarray(w, np.float32).astype(ml_dtypes.bfloat16)).reshape(k // 32, 32, n)
    amax = np.abs(w).max(1)
    if fmt == "e4m3":
        byte = np.frexp(amax)[1] - 1 + 127 - 7
    else:
        mant, ex = np.frexp(amax / 6.0)
        byte = np.where(mant > 0.5, ex, ex - 1) + 127
    byte = np.clip(np.where(amax > 0, byte, 1), 1, 254)
    scaled = (w * np.exp2(127.0 - byte)[:, None, :]).reshape(k, n).astype(np.float32)
    by_word = np.ascontiguousarray(scaled.reshape(k // 512, 128, 4, n).transpose(0, 1, 3, 2))
    if fmt == "e4m3":
        words = by_word.astype(ml_dtypes.float8_e4m3fn).view(np.uint8)
    else:
        c = by_word.astype(ml_dtypes.float4_e2m1fn).view(np.uint8) & 0xF
        words = (c[..., 0::2] | (c[..., 1::2] << 4)).reshape(k // 512, 128, 2 * n)
    return np.ascontiguousarray(words), np.ascontiguousarray(byte.astype(np.uint8).reshape(k // 512, 16, n))


def unpack_weight(words, scales, fmt):
    g, _, n = scales.shape
    words = np.ascontiguousarray(words).reshape(g, 128, n, -1)
    if fmt == "e4m3":
        vals = words.view(ml_dtypes.float8_e4m3fn).astype(np.float64)
    else:
        nib = np.empty((g, 128, n, 4), np.uint8)
        nib[..., 0::2] = words & 0xF
        nib[..., 1::2] = words >> 4
        vals = E2M1[nib]
    vals = vals * np.repeat(np.exp2(scales.astype(np.float64) - 127.0), 8, axis=1)[..., None]
    return vals.transpose(0, 1, 3, 2).reshape(g * 512, n)


def sigmoid(v):
    return 1.0 / (1.0 + np.exp(-v))


B, N, T, D, NQ = 1, 512, 2048, 1024, 128


def setup_inputs():
    n = np.random.standard_normal
    idx = np.random.permutation(T)[:B * N]
    s = mx_kscale(D)[:, None]
    kp = pack_weight(n((D, T)) / s, "e2m1")
    return {
        "qT": (n((B, D, NQ)) * s * (1.00 / np.sqrt(D))).astype(np.float32),
        "k_words": np.ascontiguousarray(kp[0].reshape(1, 2, 128, T, 2).transpose(0, 2, 3, 1, 4)).reshape(1, 128, T, 4),
        "k_scales": kp[1],
        "ag": np.tile(np.random.uniform(0.0, 40.0, 2048), (128, 1)).astype(np.float32),
        "rt": (np.random.uniform(0.01, 0.1, (B, NQ, 1))).astype(np.float32),
        "offs": striped(idx),
    }


def reference(qT, k_words, k_scales, ag, rt, offs):
    idx = unstriped(offs)
    pick = lambda x, which: x[:, which].reshape(x.shape[0], B, -1).transpose(1, 0, 2)
    k = unpack_weight(k_words.reshape(1, 128, T, 2, 2).transpose(0, 3, 1, 2, 4).reshape(2, 128, 2 * T), k_scales, "e2m1")
    kg = pick(k, idx)
    qq = mxq(f64(qT), 1, "e4m3")
    a = qq.transpose(0, 2, 1) @ kg
    y = sigmoid(a) * np.exp(-f64(rt) * pick(f64(ag), idx)[:, :1, :])
    return y

@@ -1,0 +1,123 @@
+from contextlib import ExitStack
+import math
+
+import concourse.mybir as mybir
+from concourse.masks import make_identity
+
+F32 = mybir.dt.float32
+BF16 = mybir.dt.bfloat16
+I32 = mybir.dt.int32
+U32 = mybir.dt.uint32
+U16 = mybir.dt.uint16
+U8 = mybir.dt.uint8
+FP8X4 = mybir.dt.float8_e4m3fn_x4
+FP4X4 = mybir.dt.float4_e2m1fn_x4
+ACT = mybir.ActivationFunctionType
+ALU = mybir.AluOpType
+
+P = 128
+T = 2048
+N = 512
+NQ = 128
+PASSES = 2
+PACK = 4
+AGE_ROW = 8
+FLOPS = 2 * 1024 * NQ * N
+
+
+def tile_attend_link_age_topk_kernel(tc, qT, k_words, k_scales, ag, rt, offs, out):
+    nc = tc.nc
+    with ExitStack() as ctx:
+        keep = ctx.enter_context(tc.tile_pool(name="keep", bufs=1))
+        psum = ctx.enter_context(tc.psum_pool(name="psum", bufs=1))
+
+        offsets = keep.tile([P, N // 16], U16, name="offsets")
+        nc.sync.dma_start(offsets[:], offs)
+
+        scale_pool = keep.tile([P, T], U8, name="scale_pool", align_bytes=64)
+        nc.sync.dma_start(scale_pool[0:32, :].bitcast(I32), k_scales.rearrange("o f t -> (o f) t").bitcast(I32))
+        word_pool = keep.tile([P, T], I32, name="word_pool", align_bytes=64)
+        nc.sync.dma_start(word_pool[:], k_words[0].rearrange("p t b -> p (t b)").bitcast(I32))
+        q_raw = [keep.tile([P, PACK, NQ], F32, name=f"q_raw{o}") for o in range(PASSES)]
+        for o in range(PASSES):
+            nc.sync.dma_start(q_raw[o][:], qT[0, 512 * o : 512 * (o + 1), :].rearrange("(p j) n -> p j n", j=PACK))
+
+        rate = keep.tile([P, 1], F32, name="rate")
+        nc.scalar.dma_start(rate[:], rt[0])
+        age_pool = keep.tile([P, T], F32, name="age_pool", tag="chain", align_bytes=64)
+        nc.vector.memset(age_pool[:].bitcast(I32), 0)
+        nc.scalar.dma_start(age_pool[AGE_ROW : AGE_ROW + 1, :], ag[0:1, :])
+        neg_rate = keep.tile([P, 1], F32, name="neg_rate")
+        nc.scalar.activation(neg_rate[:], rate[:], ACT.Copy, scale=-1.0)
+
+        nc.vector.memset(scale_pool[32:64, :].bitcast(I32), 0)
+        nc.vector.memset(scale_pool[64:128, :].bitcast(I32), 0)
+        k_planes = [keep.tile([P, N], U8, name=f"k_plane{o}", align_bytes=64) for o in range(PASSES)]
+        for o in range(PASSES):
+            nc.vector.memset(k_planes[o][:].bitcast(I32), 0)
+
+        ident = keep.tile([P, P], F32, name="ident")
+        make_identity(nc, ident[:])
+
+        scale_rows = keep.tile([P, N], U8, name="scale_rows", align_bytes=64)
+        nc.vector.tensor_copy(scale_rows[:], scale_pool[:].indirect(offsets[:]))
+        for o in range(PASSES):
+            for quad in range(4):
+                src = 16 * o + 4 * quad
+                nc.scalar.dma_start(
+                    k_planes[o][32 * quad : 32 * quad + 4, :].bitcast(I32),
+                    scale_rows[src : src + 4, :].bitcast(I32),
+                )
+
+        ages = keep.tile([P, N], F32, name="ages")
+        nc.vector.tensor_copy(ages[:], age_pool[:].indirect(offsets[:]))
+        turned = psum.tile([P, 4, P], F32, name="turned")
+        for c in range(4):
+            nc.tensor.transpose(turned[:, c, :], ages[:, c * P : (c + 1) * P], ident[:])
+        age_cols = keep.tile([P, 4], F32, name="age_cols")
+        nc.scalar.copy(age_cols[:], turned[:, :, AGE_ROW])
+        spread = psum.tile([P, 4, P], F32, name="spread")
+        for c in range(4):
+            nc.tensor.transpose(spread[:, c, :], age_cols[:, c : c + 1].to_broadcast([P, P]), ident[:])
+        half_decay = keep.tile([P, N], F32, name="half_decay")
+        nc.scalar.activation(
+            half_decay[:], spread[:].rearrange("p c n -> p (c n)"), ACT.Exp, scale=neg_rate[:, 0:1], bias=-math.log(2.0)
+        )
+
+        words = keep.tile([P, N], U32, name="words", tag="chain", align_bytes=64)
+        nc.vector.tensor_copy(words[:], word_pool[:].bitcast(U32).indirect(offsets[:]))
+        k_codes = keep.tile([P, PASSES, 2 * N], U8, name="k_codes", align_bytes=64)
+        nc.vector.tensor_copy(k_codes[:].bitcast(U16), words[:].bitcast(U16).rearrange("p (n h) -> p h n", h=PASSES))
+
+        q_bf = [keep.tile([P, NQ, PACK], BF16, name=f"q_bf{o}", align_bytes=64) for o in range(PASSES)]
+        q_codes = keep.tile([P, PASSES, NQ], U32, name="q_codes", tag="chain", align_bytes=64)
+        q_planes = [keep.tile([P, NQ], U8, name=f"q_plane{o}", align_bytes=64) for o in range(PASSES)]
+        for o in range(PASSES):
+            nc.scalar.copy(q_bf[o][:], q_raw[o][:].rearrange("p j n -> p n j"))
+        for o in range(PASSES):
+            nc.vector.quantize_mx(
+                out=q_codes[:, o, :].bitcast(FP8X4), scales=q_planes[o][:], in_=q_bf[o][:].rearrange("p n j -> p (n j)")
+            )
+
+        scores = [psum.tile([P, P], F32, name=f"scores{c}") for c in range(4)]
+        for o in range(PASSES):
+            for c in range(4):
+                nc.tensor.matmul_mx(
+                    out=scores[c][:],
+                    lhsT=q_codes[:, o, :].bitcast(FP8X4),
+                    lhsT_scale=q_planes[o][:],
+                    rhs=k_codes[:, o, 2 * P * c : 2 * P * (c + 1)].bitcast(FP4X4),
+                    rhs_scale=k_planes[o][:, P * c : P * (c + 1)],
+                    start=(o == 0),
+                    stop=(o == PASSES - 1),
+                )
+
+        res = [keep.tile([P, 2, P], F32, name=f"res{h}") for h in range(2)]
+        for c in range(4):
+            th = keep.tile([P, P], F32, name=f"th{c}")
+            nc.scalar.activation(th[:], scores[c][:], ACT.Tanh, scale=0.5)
+            nc.vector.scalar_tensor_tensor(
+                res[c // 2][:, c % 2, :], th[:], 1.0, half_decay[:, P * c : P * (c + 1)], ALU.add, ALU.mult
+            )
+            if c % 2 == 1:
+                nc.sync.dma_start(out[0, :, P * (c - 1) : P * (c + 1)], res[c // 2][:].rearrange("p a n -> p (a n)"))

@@ -21,7 +21,8 @@ N = 512
 NQ = 128
 PASSES = 2
 PACK = 4
-AGE_ROW = 8
+AGE_ROW = 127
+SCALE_ROW0 = 96
 FLOPS = 2 * 1024 * NQ * N
 
 
@@ -29,32 +30,30 @@ def tile_attend_link_age_topk_kernel(tc, qT, k_words, k_scales, ag, rt, offs, ou
     nc = tc.nc
     with ExitStack() as ctx:
         keep = ctx.enter_context(tc.tile_pool(name="keep", bufs=1))
+        shared = ctx.enter_context(tc.tile_pool(name="shared", bufs=1))
         psum = ctx.enter_context(tc.psum_pool(name="psum", bufs=1))
 
         offsets = keep.tile([P, N // 16], U16, name="offsets")
         nc.sync.dma_start(offsets[:], offs)
-
         scale_pool = keep.tile([P, T], U8, name="scale_pool", align_bytes=64)
-        nc.sync.dma_start(scale_pool[0:32, :].bitcast(I32), k_scales.rearrange("o f t -> (o f) t").bitcast(I32))
-        word_pool = keep.tile([P, T], I32, name="word_pool", align_bytes=64)
+        nc.sync.dma_start(scale_pool[SCALE_ROW0:P, :].bitcast(I32), k_scales.rearrange("o f t -> (o f) t").bitcast(I32))
+        age_pool = keep.tile([P, T], F32, name="age_pool", align_bytes=64)
+        nc.sync.dma_start(age_pool[AGE_ROW:P, :], ag[0:1, :])
+        word_pool = shared.tile([P, T], I32, name="word_pool", offset=0, align_bytes=64)
         nc.sync.dma_start(word_pool[:], k_words[0].rearrange("p t b -> p (t b)").bitcast(I32))
         q_raw = [keep.tile([P, PACK, NQ], F32, name=f"q_raw{o}") for o in range(PASSES)]
         for o in range(PASSES):
             nc.sync.dma_start(q_raw[o][:], qT[0, 512 * o : 512 * (o + 1), :].rearrange("(p j) n -> p j n", j=PACK))
-
         rate = keep.tile([P, 1], F32, name="rate")
         nc.scalar.dma_start(rate[:], rt[0])
-        age_pool = keep.tile([P, T], F32, name="age_pool", tag="chain", align_bytes=64)
-        nc.vector.memset(age_pool[:].bitcast(I32), 0)
-        nc.scalar.dma_start(age_pool[AGE_ROW : AGE_ROW + 1, :], ag[0:1, :])
         neg_rate = keep.tile([P, 1], F32, name="neg_rate")
         nc.scalar.activation(neg_rate[:], rate[:], ACT.Copy, scale=-1.0)
 
-        nc.vector.memset(scale_pool[32:64, :].bitcast(I32), 0)
-        nc.vector.memset(scale_pool[64:128, :].bitcast(I32), 0)
-        k_planes = [keep.tile([P, N], U8, name=f"k_plane{o}", align_bytes=64) for o in range(PASSES)]
-        for o in range(PASSES):
-            nc.vector.memset(k_planes[o][:].bitcast(I32), 0)
+        nc.vector.memset(scale_pool[0:SCALE_ROW0, :].bitcast(I32), 0)
+        k_planes = keep.tile([P, PASSES, N], U8, name="k_planes", align_bytes=64)
+        nc.vector.memset(k_planes[:].rearrange("p o n -> p (o n)").bitcast(I32), 0)
+        nc.gpsimd.memset(age_pool[0:AGE_ROW, 0:768].bitcast(I32), 0)
+        nc.vector.memset(age_pool[0:AGE_ROW, 768:T].bitcast(I32), 0)
 
         ident = keep.tile([P, P], F32, name="ident")
         make_identity(nc, ident[:])
@@ -63,41 +62,47 @@ def tile_attend_link_age_topk_kernel(tc, qT, k_words, k_scales, ag, rt, offs, ou
         nc.vector.tensor_copy(scale_rows[:], scale_pool[:].indirect(offsets[:]))
         for o in range(PASSES):
             for quad in range(4):
-                src = 16 * o + 4 * quad
-                nc.scalar.dma_start(
-                    k_planes[o][32 * quad : 32 * quad + 4, :].bitcast(I32),
+                src = SCALE_ROW0 + 16 * o + 4 * quad
+                queue = nc.gpsimd if (o, quad) == (PASSES - 1, 3) else nc.sync
+                queue.dma_start(
+                    k_planes[32 * quad : 32 * quad + 4, o, :].bitcast(I32),
                     scale_rows[src : src + 4, :].bitcast(I32),
                 )
 
-        ages = keep.tile([P, N], F32, name="ages")
-        nc.vector.tensor_copy(ages[:], age_pool[:].indirect(offsets[:]))
-        turned = psum.tile([P, 4, P], F32, name="turned")
-        for c in range(4):
-            nc.tensor.transpose(turned[:, c, :], ages[:, c * P : (c + 1) * P], ident[:])
-        age_cols = keep.tile([P, 4], F32, name="age_cols")
-        nc.scalar.copy(age_cols[:], turned[:, :, AGE_ROW])
+        ages = [shared.tile([P, N // 2], F32, name=f"ages{h}", offset=4 * T + 2 * N * h, align_bytes=64) for h in range(2)]
+        turned = [psum.tile([P, 2, P], F32, name=f"turned{h}") for h in range(2)]
+        for h in range(2):
+            nc.vector.tensor_copy(ages[h][:], age_pool[:].indirect(offsets[:, 16 * h : 16 * (h + 1)]))
+            for c in range(2):
+                nc.tensor.transpose(turned[h][:, c, :], ages[h][:, c * P : (c + 1) * P], ident[:])
+
+        words = keep.tile([P, N], U32, name="words", align_bytes=64)
+        nc.vector.tensor_copy(words[:], word_pool[:].bitcast(U32).indirect(offsets[:]))
+
         spread = psum.tile([P, 4, P], F32, name="spread")
-        for c in range(4):
-            nc.tensor.transpose(spread[:, c, :], age_cols[:, c : c + 1].to_broadcast([P, P]), ident[:])
+        q_bf = [shared.tile([P, NQ, PACK], BF16, name=f"q_bf{o}", offset=4 * T + 2 * N * o, align_bytes=64) for o in range(PASSES)]
+        for h in range(2):
+            age_cols = keep.tile([P, 2], F32, name=f"age_cols{h}")
+            nc.scalar.copy(age_cols[:], turned[h][:, :, AGE_ROW])
+            for c in range(2):
+                nc.tensor.transpose(spread[:, 2 * h + c, :], age_cols[:, c : c + 1].to_broadcast([P, P]), ident[:])
+            nc.scalar.copy(q_bf[h][:], q_raw[h][:].rearrange("p j n -> p n j"))
+
+        q_codes = shared.tile([P, PASSES, NQ], U32, name="q_codes", offset=0, align_bytes=64)
+        q_planes = [keep.tile([P, NQ], U8, name=f"q_plane{o}", align_bytes=64) for o in range(PASSES)]
+        k_codes = [keep.tile([P, 2 * N], U8, name=f"k_codes{o}", align_bytes=64) for o in range(PASSES)]
+        for o in range(PASSES):
+            nc.vector.tensor_copy(
+                k_codes[o][:].bitcast(U16), words[:].bitcast(U16).rearrange("p (n o) -> p o n", o=PASSES)[:, o, :]
+            )
+            nc.vector.quantize_mx(
+                out=q_codes[:, o, :].bitcast(FP8X4), scales=q_planes[o][:], in_=q_bf[o][:].rearrange("p n j -> p (n j)")
+            )
+
         half_decay = keep.tile([P, N], F32, name="half_decay")
         nc.scalar.activation(
             half_decay[:], spread[:].rearrange("p c n -> p (c n)"), ACT.Exp, scale=neg_rate[:, 0:1], bias=-math.log(2.0)
         )
-
-        words = keep.tile([P, N], U32, name="words", tag="chain", align_bytes=64)
-        nc.vector.tensor_copy(words[:], word_pool[:].bitcast(U32).indirect(offsets[:]))
-        k_codes = keep.tile([P, PASSES, 2 * N], U8, name="k_codes", align_bytes=64)
-        nc.vector.tensor_copy(k_codes[:].bitcast(U16), words[:].bitcast(U16).rearrange("p (n h) -> p h n", h=PASSES))
-
-        q_bf = [keep.tile([P, NQ, PACK], BF16, name=f"q_bf{o}", align_bytes=64) for o in range(PASSES)]
-        q_codes = keep.tile([P, PASSES, NQ], U32, name="q_codes", tag="chain", align_bytes=64)
-        q_planes = [keep.tile([P, NQ], U8, name=f"q_plane{o}", align_bytes=64) for o in range(PASSES)]
-        for o in range(PASSES):
-            nc.scalar.copy(q_bf[o][:], q_raw[o][:].rearrange("p j n -> p n j"))
-        for o in range(PASSES):
-            nc.vector.quantize_mx(
-                out=q_codes[:, o, :].bitcast(FP8X4), scales=q_planes[o][:], in_=q_bf[o][:].rearrange("p n j -> p (n j)")
-            )
 
         scores = [psum.tile([P, P], F32, name=f"scores{c}") for c in range(4)]
         for o in range(PASSES):
@@ -106,8 +111,8 @@ def tile_attend_link_age_topk_kernel(tc, qT, k_words, k_scales, ag, rt, offs, ou
                     out=scores[c][:],
                     lhsT=q_codes[:, o, :].bitcast(FP8X4),
                     lhsT_scale=q_planes[o][:],
-                    rhs=k_codes[:, o, 2 * P * c : 2 * P * (c + 1)].bitcast(FP4X4),
-                    rhs_scale=k_planes[o][:, P * c : P * (c + 1)],
+                    rhs=k_codes[o][:, 2 * P * c : 2 * P * (c + 1)].bitcast(FP4X4),
+                    rhs_scale=k_planes[:, o, P * c : P * (c + 1)],
                     start=(o == 0),
                     stop=(o == PASSES - 1),
                 )

@@ -22,7 +22,6 @@ NQ = 128
 PASSES = 2
 PACK = 4
 AGE_ROW = 127
-SCALE_ROW0 = 96
 FLOPS = 2 * 1024 * NQ * N
 
 
@@ -35,87 +34,96 @@ def tile_attend_link_age_topk_kernel(tc, qT, k_words, k_scales, ag, rt, offs, ou
 
         offsets = keep.tile([P, N // 16], U16, name="offsets")
         nc.sync.dma_start(offsets[:], offs)
-        scale_pool = keep.tile([P, T], U8, name="scale_pool", align_bytes=64)
-        nc.sync.dma_start(scale_pool[SCALE_ROW0:P, :].bitcast(I32), k_scales.rearrange("o f t -> (o f) t").bitcast(I32))
-        age_pool = keep.tile([P, T], F32, name="age_pool", align_bytes=64)
+        scale_pool = keep.tile([P, T + 64], U8, name="scale_pool", align_bytes=64)
+        scale_src = k_scales.bitcast(I32).rearrange("o (h e j) t -> e (o h) j t", e=2, j=4)
+        for e in range(2):
+            nc.sync.dma_start(scale_pool[32 * e + 16 : 32 * e + 32, 0:T].bitcast(I32), scale_src[e])
+        age_pool = shared.tile([P, T], F32, name="age_pool", offset=0, align_bytes=64)
         nc.sync.dma_start(age_pool[AGE_ROW:P, :], ag[0:1, :])
-        word_pool = shared.tile([P, T], I32, name="word_pool", offset=0, align_bytes=64)
-        nc.sync.dma_start(word_pool[:], k_words[0].rearrange("p t b -> p (t b)").bitcast(I32))
+        word_pool = shared.tile([P, T], I32, name="word_pool", offset=4 * T, align_bytes=64)
         q_raw = [keep.tile([P, PACK, NQ], F32, name=f"q_raw{o}") for o in range(PASSES)]
-        for o in range(PASSES):
-            nc.sync.dma_start(q_raw[o][:], qT[0, 512 * o : 512 * (o + 1), :].rearrange("(p j) n -> p j n", j=PACK))
+        q_rows = qT[0].rearrange("(o p j) n -> o p j n", o=PASSES, j=PACK)
+        nc.sync.dma_start(q_raw[0][:], q_rows[0])
+        nc.sync.dma_start(word_pool[:], k_words[0].rearrange("p t b -> p (t b)").bitcast(I32))
+        nc.sync.dma_start(q_raw[1][:], q_rows[1])
         rate = keep.tile([P, 1], F32, name="rate")
-        nc.scalar.dma_start(rate[:], rt[0])
-        neg_rate = keep.tile([P, 1], F32, name="neg_rate")
-        nc.scalar.activation(neg_rate[:], rate[:], ACT.Copy, scale=-1.0)
+        nc.sync.dma_start(rate[:], rt[0])
 
-        nc.vector.memset(scale_pool[0:SCALE_ROW0, :].bitcast(I32), 0)
-        k_planes = keep.tile([P, PASSES, N], U8, name="k_planes", align_bytes=64)
-        nc.vector.memset(k_planes[:].rearrange("p o n -> p (o n)").bitcast(I32), 0)
-        nc.gpsimd.memset(age_pool[0:AGE_ROW, 0:768].bitcast(I32), 0)
-        nc.vector.memset(age_pool[0:AGE_ROW, 768:T].bitcast(I32), 0)
-
+        for lo, hi in ((0, 16), (32, 48), (64, P)):
+            nc.vector.memset(scale_pool[lo:hi, 0 : T + 4].bitcast(I32), 0)
         ident = keep.tile([P, P], F32, name="ident")
         make_identity(nc, ident[:])
+        nc.gpsimd.memset(age_pool[0:AGE_ROW, :].bitcast(I32), 0)
 
         scale_rows = keep.tile([P, N], U8, name="scale_rows", align_bytes=64)
-        nc.vector.tensor_copy(scale_rows[:], scale_pool[:].indirect(offsets[:]))
+        nc.vector.tensor_copy(scale_rows[:], scale_pool[:, 0:T].indirect(offsets[:]))
+        k_planes = keep.tile([P, PASSES, N], U8, name="k_planes", align_bytes=64)
         for o in range(PASSES):
-            for quad in range(4):
-                src = SCALE_ROW0 + 16 * o + 4 * quad
-                queue = nc.gpsimd if (o, quad) == (PASSES - 1, 3) else nc.sync
-                queue.dma_start(
-                    k_planes[32 * quad : 32 * quad + 4, o, :].bitcast(I32),
-                    scale_rows[src : src + 4, :].bitcast(I32),
+            for h in range(2):
+                src = 16 + 4 * (2 * o + h)
+                nc.sync.dma_start(
+                    k_planes[64 * h : 64 * (h + 1), o, :].bitcast(I32),
+                    scale_rows[src : src + 64, :].bitcast(I32),
                 )
 
-        ages = [shared.tile([P, N // 2], F32, name=f"ages{h}", offset=4 * T + 2 * N * h, align_bytes=64) for h in range(2)]
+        ages0 = keep.tile([P, N // 2], F32, name="ages0")
+        ages1 = shared.tile([P, N // 2], F32, name="ages1", offset=8 * T, align_bytes=64)
+        ages = [ages0, ages1]
         turned = [psum.tile([P, 2, P], F32, name=f"turned{h}") for h in range(2)]
         for h in range(2):
             nc.vector.tensor_copy(ages[h][:], age_pool[:].indirect(offsets[:, 16 * h : 16 * (h + 1)]))
             for c in range(2):
                 nc.tensor.transpose(turned[h][:, c, :], ages[h][:, c * P : (c + 1) * P], ident[:])
 
-        words = keep.tile([P, N], U32, name="words", align_bytes=64)
-        nc.vector.tensor_copy(words[:], word_pool[:].bitcast(U32).indirect(offsets[:]))
-
         spread = psum.tile([P, 4, P], F32, name="spread")
-        q_bf = [shared.tile([P, NQ, PACK], BF16, name=f"q_bf{o}", offset=4 * T + 2 * N * o, align_bytes=64) for o in range(PASSES)]
+        q_bf0 = keep.tile([P, NQ, PACK], BF16, name="q_bf0", align_bytes=64)
+        q_bf1 = shared.tile([P, NQ, PACK], BF16, name="q_bf1", offset=8 * T, align_bytes=64)
+        q_bf = [q_bf0, q_bf1]
         for h in range(2):
             age_cols = keep.tile([P, 2], F32, name=f"age_cols{h}")
-            nc.scalar.copy(age_cols[:], turned[h][:, :, AGE_ROW])
+            nc.scalar.activation(age_cols[:], turned[h][:, :, AGE_ROW], ACT.Copy, scale=-1.0)
             for c in range(2):
                 nc.tensor.transpose(spread[:, 2 * h + c, :], age_cols[:, c : c + 1].to_broadcast([P, P]), ident[:])
-            nc.scalar.copy(q_bf[h][:], q_raw[h][:].rearrange("p j n -> p n j"))
+            nc.scalar.activation(q_bf[h][:], q_raw[h][:].rearrange("p j n -> p n j"), ACT.Copy)
 
-        q_codes = shared.tile([P, PASSES, NQ], U32, name="q_codes", offset=0, align_bytes=64)
+        q_codes = [shared.tile([P, NQ], U32, name=f"q_codes{o}", offset=4 * T * o, align_bytes=64) for o in range(PASSES)]
         q_planes = [keep.tile([P, NQ], U8, name=f"q_plane{o}", align_bytes=64) for o in range(PASSES)]
-        k_codes = [keep.tile([P, 2 * N], U8, name=f"k_codes{o}", align_bytes=64) for o in range(PASSES)]
-        for o in range(PASSES):
-            nc.vector.tensor_copy(
-                k_codes[o][:].bitcast(U16), words[:].bitcast(U16).rearrange("p (n o) -> p o n", o=PASSES)[:, o, :]
-            )
+        words = [keep.tile([P, N // 2], U32, name=f"words{h}", align_bytes=64) for h in range(2)]
+        k_codes = [keep.tile([P, PASSES, N], U8, name=f"k_codes{h}", align_bytes=64) for h in range(2)]
+
+        def quantize(o):
             nc.vector.quantize_mx(
-                out=q_codes[:, o, :].bitcast(FP8X4), scales=q_planes[o][:], in_=q_bf[o][:].rearrange("p n j -> p (n j)")
+                out=q_codes[o][:].bitcast(FP8X4), scales=q_planes[o][:], in_=q_bf[o][:].rearrange("p n j -> p (n j)")
             )
+
+        def split(h):
+            nc.vector.tensor_copy(
+                k_codes[h][:].bitcast(U16), words[h][:].bitcast(U16).rearrange("p (n o) -> p o n", o=PASSES)
+            )
+
+        quantize(0)
+        for h in range(2):
+            nc.vector.tensor_copy(words[h][:], word_pool[:].bitcast(U32).indirect(offsets[:, 16 * h : 16 * (h + 1)]))
+        split(0)
+        quantize(1)
+        split(1)
 
         half_decay = keep.tile([P, N], F32, name="half_decay")
         nc.scalar.activation(
-            half_decay[:], spread[:].rearrange("p c n -> p (c n)"), ACT.Exp, scale=neg_rate[:, 0:1], bias=-math.log(2.0)
+            half_decay[:], spread[:].rearrange("p c n -> p (c n)"), ACT.Exp, scale=rate[:, 0:1], bias=-math.log(2.0)
         )
 
         scores = [psum.tile([P, P], F32, name=f"scores{c}") for c in range(4)]
-        for o in range(PASSES):
-            for c in range(4):
-                nc.tensor.matmul_mx(
-                    out=scores[c][:],
-                    lhsT=q_codes[:, o, :].bitcast(FP8X4),
-                    lhsT_scale=q_planes[o][:],
-                    rhs=k_codes[o][:, 2 * P * c : 2 * P * (c + 1)].bitcast(FP4X4),
-                    rhs_scale=k_planes[:, o, P * c : P * (c + 1)],
-                    start=(o == 0),
-                    stop=(o == PASSES - 1),
-                )
+        for c, o in [(0, 0), (1, 0), (0, 1), (1, 1), (2, 0), (2, 1), (3, 0), (3, 1)]:
+            nc.tensor.matmul_mx(
+                out=scores[c][:],
+                lhsT=q_codes[o][:].bitcast(FP8X4),
+                lhsT_scale=q_planes[o][:],
+                rhs=k_codes[c // 2][:, o, 2 * P * (c % 2) : 2 * P * (c % 2 + 1)].bitcast(FP4X4),
+                rhs_scale=k_planes[:, o, P * c : P * (c + 1)],
+                start=(o == 0),
+                stop=(o == PASSES - 1),
+            )
 
         res = [keep.tile([P, 2, P], F32, name=f"res{h}") for h in range(2)]
         for c in range(4):

@@ -38,9 +38,9 @@ def tile_attend_link_age_topk_kernel(tc, qT, k_words, k_scales, ag, rt, offs, ou
         scale_src = k_scales.bitcast(I32).rearrange("o (h e j) t -> e (o h) j t", e=2, j=4)
         for e in range(2):
             nc.sync.dma_start(scale_pool[32 * e + 16 : 32 * e + 32, 0:T].bitcast(I32), scale_src[e])
-        age_pool = shared.tile([P, T], F32, name="age_pool", offset=0, align_bytes=64)
+        age_pool = keep.tile([P, T], F32, name="age_pool", align_bytes=64)
         nc.sync.dma_start(age_pool[AGE_ROW:P, :], ag[0:1, :])
-        word_pool = shared.tile([P, T], I32, name="word_pool", offset=4 * T, align_bytes=64)
+        word_pool = shared.tile([P, T], I32, name="word_pool", offset=0, align_bytes=64)
         q_raw = [keep.tile([P, PACK, NQ], F32, name=f"q_raw{o}") for o in range(PASSES)]
         q_rows = qT[0].rearrange("(o p j) n -> o p j n", o=PASSES, j=PACK)
         nc.sync.dma_start(q_raw[0][:], q_rows[0])
@@ -67,7 +67,7 @@ def tile_attend_link_age_topk_kernel(tc, qT, k_words, k_scales, ag, rt, offs, ou
                 )
 
         ages0 = keep.tile([P, N // 2], F32, name="ages0")
-        ages1 = shared.tile([P, N // 2], F32, name="ages1", offset=8 * T, align_bytes=64)
+        ages1 = shared.tile([P, N // 2], F32, name="ages1", offset=4 * T, align_bytes=64)
         ages = [ages0, ages1]
         turned = [psum.tile([P, 2, P], F32, name=f"turned{h}") for h in range(2)]
         for h in range(2):
@@ -77,16 +77,22 @@ def tile_attend_link_age_topk_kernel(tc, qT, k_words, k_scales, ag, rt, offs, ou
 
         spread = psum.tile([P, 4, P], F32, name="spread")
         q_bf0 = keep.tile([P, NQ, PACK], BF16, name="q_bf0", align_bytes=64)
-        q_bf1 = shared.tile([P, NQ, PACK], BF16, name="q_bf1", offset=8 * T, align_bytes=64)
+        q_bf1 = shared.tile([P, NQ, PACK], BF16, name="q_bf1", offset=4 * T, align_bytes=64)
         q_bf = [q_bf0, q_bf1]
         for h in range(2):
             age_cols = keep.tile([P, 2], F32, name=f"age_cols{h}")
             nc.scalar.activation(age_cols[:], turned[h][:, :, AGE_ROW], ACT.Copy, scale=-1.0)
             for c in range(2):
                 nc.tensor.transpose(spread[:, 2 * h + c, :], age_cols[:, c : c + 1].to_broadcast([P, P]), ident[:])
-            nc.scalar.activation(q_bf[h][:], q_raw[h][:].rearrange("p j n -> p n j"), ACT.Copy)
+            nc.scalar.activation(
+                q_bf[h][:].rearrange("p (c i) j -> p c j i", i=4),
+                q_raw[h][:].rearrange("p j (c i) -> p c j i", i=4),
+                ACT.Copy,
+            )
 
-        q_codes = [shared.tile([P, NQ], U32, name=f"q_codes{o}", offset=4 * T * o, align_bytes=64) for o in range(PASSES)]
+        q_codes0 = keep.tile([P, NQ], U32, name="q_codes0", align_bytes=64)
+        q_codes1 = shared.tile([P, NQ], U32, name="q_codes1", offset=0, align_bytes=64)
+        q_codes = [q_codes0, q_codes1]
         q_planes = [keep.tile([P, NQ], U8, name=f"q_plane{o}", align_bytes=64) for o in range(PASSES)]
         words = [keep.tile([P, N // 2], U32, name=f"words{h}", align_bytes=64) for h in range(2)]
         k_codes = [keep.tile([P, PASSES, N], U8, name=f"k_codes{h}", align_bytes=64) for h in range(2)]

@@ -22,6 +22,7 @@ NQ = 128
 PASSES = 2
 PACK = 4
 AGE_ROW = 127
+AGE_SPLIT = 768
 FLOPS = 2 * 1024 * NQ * N
 
 
@@ -34,39 +35,39 @@ def tile_attend_link_age_topk_kernel(tc, qT, k_words, k_scales, ag, rt, offs, ou
 
         offsets = keep.tile([P, N // 16], U16, name="offsets")
         nc.sync.dma_start(offsets[:], offs)
-        scale_pool = keep.tile([P, T + 64], U8, name="scale_pool", align_bytes=64)
-        scale_src = k_scales.bitcast(I32).rearrange("o (h e j) t -> e (o h) j t", e=2, j=4)
-        for e in range(2):
-            nc.sync.dma_start(scale_pool[32 * e + 16 : 32 * e + 32, 0:T].bitcast(I32), scale_src[e])
+        scale_pool = keep.tile([P, T], U8, name="scale_pool", align_bytes=64)
+        nc.sync.dma_start(scale_pool[96:P, :].bitcast(I32), k_scales.bitcast(I32).rearrange("o f t -> f o t"))
         age_pool = keep.tile([P, T], F32, name="age_pool", align_bytes=64)
         nc.sync.dma_start(age_pool[AGE_ROW:P, :], ag[0:1, :])
         word_pool = shared.tile([P, T], I32, name="word_pool", offset=0, align_bytes=64)
+        nc.sync.dma_start(word_pool[:], k_words[0].rearrange("p t b -> p (t b)").bitcast(I32))
         q_raw = [keep.tile([P, PACK, NQ], F32, name=f"q_raw{o}") for o in range(PASSES)]
         q_rows = qT[0].rearrange("(o p j) n -> o p j n", o=PASSES, j=PACK)
-        nc.sync.dma_start(q_raw[0][:], q_rows[0])
-        nc.sync.dma_start(word_pool[:], k_words[0].rearrange("p t b -> p (t b)").bitcast(I32))
-        nc.sync.dma_start(q_raw[1][:], q_rows[1])
+        for o in range(PASSES):
+            nc.sync.dma_start(q_raw[o][:], q_rows[o])
         rate = keep.tile([P, 1], F32, name="rate")
         nc.sync.dma_start(rate[:], rt[0])
 
-        for lo, hi in ((0, 16), (32, 48), (64, P)):
-            nc.vector.memset(scale_pool[lo:hi, 0 : T + 4].bitcast(I32), 0)
+        k_planes = keep.tile([P, PASSES * N], U8, name="k_planes", align_bytes=64)
+        scale_words = scale_pool[0:96, :].bitcast(I32)
+        age_words = age_pool[0:AGE_ROW, :].bitcast(I32)
+        plane_words = k_planes[:].bitcast(I32)
+        for region, lo, mid, hi in ((scale_words, 0, 255, 512), (age_words, 0, 511, AGE_SPLIT), (plane_words, 0, 127, 256)):
+            nc.vector.memset(region[:, lo:mid], 0)
+            nc.vector.memset(region[:, mid:hi], 0)
+        nc.gpsimd.memset(age_words[:, AGE_SPLIT:T], 0)
         ident = keep.tile([P, P], F32, name="ident")
         make_identity(nc, ident[:])
-        nc.gpsimd.memset(age_pool[0:AGE_ROW, :].bitcast(I32), 0)
 
         scale_rows = keep.tile([P, N], U8, name="scale_rows", align_bytes=64)
-        nc.vector.tensor_copy(scale_rows[:], scale_pool[:, 0:T].indirect(offsets[:]))
-        k_planes = keep.tile([P, PASSES, N], U8, name="k_planes", align_bytes=64)
-        for o in range(PASSES):
-            for h in range(2):
-                src = 16 + 4 * (2 * o + h)
-                nc.sync.dma_start(
-                    k_planes[64 * h : 64 * (h + 1), o, :].bitcast(I32),
-                    scale_rows[src : src + 64, :].bitcast(I32),
-                )
+        nc.vector.tensor_copy(scale_rows[:], scale_pool[:].indirect(offsets[:]))
+        for quad in range(4):
+            nc.sync.dma_start(
+                k_planes[32 * quad : 32 * quad + 4, :].bitcast(I32),
+                scale_rows[96 + 8 * quad : 96 + 8 * (quad + 1), :].bitcast(I32),
+            )
 
-        ages0 = keep.tile([P, N // 2], F32, name="ages0")
+        ages0 = shared.tile([P, N // 2], F32, name="ages0", offset=4 * T + 1024, align_bytes=64)
         ages1 = shared.tile([P, N // 2], F32, name="ages1", offset=4 * T, align_bytes=64)
         ages = [ages0, ages1]
         turned = [psum.tile([P, 2, P], F32, name=f"turned{h}") for h in range(2)]
@@ -76,7 +77,7 @@ def tile_attend_link_age_topk_kernel(tc, qT, k_words, k_scales, ag, rt, offs, ou
                 nc.tensor.transpose(turned[h][:, c, :], ages[h][:, c * P : (c + 1) * P], ident[:])
 
         spread = psum.tile([P, 4, P], F32, name="spread")
-        q_bf0 = keep.tile([P, NQ, PACK], BF16, name="q_bf0", align_bytes=64)
+        q_bf0 = shared.tile([P, NQ, PACK], BF16, name="q_bf0", offset=4 * T + 1024, align_bytes=64)
         q_bf1 = shared.tile([P, NQ, PACK], BF16, name="q_bf1", offset=4 * T, align_bytes=64)
         q_bf = [q_bf0, q_bf1]
         for h in range(2):
@@ -90,7 +91,7 @@ def tile_attend_link_age_topk_kernel(tc, qT, k_words, k_scales, ag, rt, offs, ou
                 ACT.Copy,
             )
 
-        q_codes0 = keep.tile([P, NQ], U32, name="q_codes0", align_bytes=64)
+        q_codes0 = shared.tile([P, NQ], U32, name="q_codes0", offset=512, align_bytes=64)
         q_codes1 = shared.tile([P, NQ], U32, name="q_codes1", offset=0, align_bytes=64)
         q_codes = [q_codes0, q_codes1]
         q_planes = [keep.tile([P, NQ], U8, name=f"q_plane{o}", align_bytes=64) for o in range(PASSES)]
@@ -107,12 +108,12 @@ def tile_attend_link_age_topk_kernel(tc, qT, k_words, k_scales, ag, rt, offs, ou
                 k_codes[h][:].bitcast(U16), words[h][:].bitcast(U16).rearrange("p (n o) -> p o n", o=PASSES)
             )
 
-        quantize(0)
         for h in range(2):
             nc.vector.tensor_copy(words[h][:], word_pool[:].bitcast(U32).indirect(offsets[:, 16 * h : 16 * (h + 1)]))
         split(0)
-        quantize(1)
+        quantize(0)
         split(1)
+        quantize(1)
 
         half_decay = keep.tile([P, N], F32, name="half_decay")
         nc.scalar.activation(
@@ -120,13 +121,13 @@ def tile_attend_link_age_topk_kernel(tc, qT, k_words, k_scales, ag, rt, offs, ou
         )
 
         scores = [psum.tile([P, P], F32, name=f"scores{c}") for c in range(4)]
-        for c, o in [(0, 0), (1, 0), (0, 1), (1, 1), (2, 0), (2, 1), (3, 0), (3, 1)]:
+        for c, o in [(c, o) for o in range(PASSES) for c in range(4)]:
             nc.tensor.matmul_mx(
                 out=scores[c][:],
                 lhsT=q_codes[o][:].bitcast(FP8X4),
                 lhsT_scale=q_planes[o][:],
                 rhs=k_codes[c // 2][:, o, 2 * P * (c % 2) : 2 * P * (c % 2 + 1)].bitcast(FP4X4),
-                rhs_scale=k_planes[:, o, P * c : P * (c + 1)],
+                rhs_scale=k_planes[:, o * N + P * c : o * N + P * (c + 1)],
                 start=(o == 0),
                 stop=(o == PASSES - 1),
             )

@@ -36,7 +36,7 @@ def tile_attend_link_age_topk_kernel(tc, qT, k_words, k_scales, ag, rt, offs, ou
         offsets = keep.tile([P, N // 16], U16, name="offsets")
         nc.sync.dma_start(offsets[:], offs)
         scale_pool = keep.tile([P, T], U8, name="scale_pool", align_bytes=64)
-        nc.sync.dma_start(scale_pool[96:P, :].bitcast(I32), k_scales.bitcast(I32).rearrange("o f t -> f o t"))
+        nc.scalar.dma_start(scale_pool[96:P, :].bitcast(I32), k_scales.bitcast(I32).rearrange("o f t -> f o t"))
         age_pool = keep.tile([P, T], F32, name="age_pool", align_bytes=64)
         nc.sync.dma_start(age_pool[AGE_ROW:P, :], ag[0:1, :])
         word_pool = shared.tile([P, T], I32, name="word_pool", offset=0, align_bytes=64)
@@ -92,27 +92,30 @@ def tile_attend_link_age_topk_kernel(tc, qT, k_words, k_scales, ag, rt, offs, ou
             )
 
         q_codes0 = shared.tile([P, NQ], U32, name="q_codes0", offset=512, align_bytes=64)
-        q_codes1 = shared.tile([P, NQ], U32, name="q_codes1", offset=0, align_bytes=64)
+        q_codes1 = shared.tile([P, NQ], U32, name="q_codes1", offset=4 * T + 2048, align_bytes=64)
         q_codes = [q_codes0, q_codes1]
         q_planes = [keep.tile([P, NQ], U8, name=f"q_plane{o}", align_bytes=64) for o in range(PASSES)]
-        words = [keep.tile([P, N // 2], U32, name=f"words{h}", align_bytes=64) for h in range(2)]
-        k_codes = [keep.tile([P, PASSES, N], U8, name=f"k_codes{h}", align_bytes=64) for h in range(2)]
+        words0 = shared.tile([P, N // 2], U32, name="words0", offset=4 * T + 2048, align_bytes=64)
+        words1 = keep.tile([P, N // 2], U32, name="words1", align_bytes=64)
+        words = [words0, words1]
+        k_first = [keep.tile([P, PASSES, 2 * P], U8, name=f"k_first{c}", align_bytes=64) for c in range(2)]
+        k_last = keep.tile([P, PASSES, N], U8, name="k_last", align_bytes=64)
+        k_codes = [k_first[0][:], k_first[1][:], k_last[:, :, 0 : 2 * P], k_last[:, :, 2 * P : N]]
 
         def quantize(o):
             nc.vector.quantize_mx(
                 out=q_codes[o][:].bitcast(FP8X4), scales=q_planes[o][:], in_=q_bf[o][:].rearrange("p n j -> p (n j)")
             )
 
-        def split(h):
-            nc.vector.tensor_copy(
-                k_codes[h][:].bitcast(U16), words[h][:].bitcast(U16).rearrange("p (n o) -> p o n", o=PASSES)
-            )
+        def split(dst, src):
+            nc.vector.tensor_copy(dst.bitcast(U16), src.bitcast(U16).rearrange("p (n o) -> p o n", o=PASSES))
 
         for h in range(2):
             nc.vector.tensor_copy(words[h][:], word_pool[:].bitcast(U32).indirect(offsets[:, 16 * h : 16 * (h + 1)]))
-        split(0)
+        split(k_first[0][:], words0[:, 0:P])
         quantize(0)
-        split(1)
+        split(k_first[1][:], words0[:, P : 2 * P])
+        split(k_last[:], words1[:])
         quantize(1)
 
         half_decay = keep.tile([P, N], F32, name="half_decay")
@@ -126,18 +129,22 @@ def tile_attend_link_age_topk_kernel(tc, qT, k_words, k_scales, ag, rt, offs, ou
                 out=scores[c][:],
                 lhsT=q_codes[o][:].bitcast(FP8X4),
                 lhsT_scale=q_planes[o][:],
-                rhs=k_codes[c // 2][:, o, 2 * P * (c % 2) : 2 * P * (c % 2 + 1)].bitcast(FP4X4),
+                rhs=k_codes[c][:, o, :].bitcast(FP4X4),
                 rhs_scale=k_planes[:, o * N + P * c : o * N + P * (c + 1)],
                 start=(o == 0),
                 stop=(o == PASSES - 1),
             )
 
-        res = [keep.tile([P, 2, P], F32, name=f"res{h}") for h in range(2)]
+        res_first = keep.tile([P, 2 * P], F32, name="res_first")
+        res_last = [keep.tile([P, P], F32, name=f"res_last{c}") for c in range(2)]
+        res = [res_first[:, 0:P], res_first[:, P : 2 * P], res_last[0][:], res_last[1][:]]
         for c in range(4):
             th = keep.tile([P, P], F32, name=f"th{c}")
             nc.scalar.activation(th[:], scores[c][:], ACT.Tanh, scale=0.5)
             nc.vector.scalar_tensor_tensor(
-                res[c // 2][:, c % 2, :], th[:], 1.0, half_decay[:, P * c : P * (c + 1)], ALU.add, ALU.mult
+                res[c], th[:], 1.0, half_decay[:, P * c : P * (c + 1)], ALU.add, ALU.mult
             )
-            if c % 2 == 1:
-                nc.sync.dma_start(out[0, :, P * (c - 1) : P * (c + 1)], res[c // 2][:].rearrange("p a n -> p (a n)"))
+            if c == 1:
+                nc.sync.dma_start(out[0, :, 0 : 2 * P], res_first[:])
+            elif c > 1:
+                nc.sync.dma_start(out[0, :, P * c : P * (c + 1)], res[c])

@@ -36,15 +36,15 @@ def tile_attend_link_age_topk_kernel(tc, qT, k_words, k_scales, ag, rt, offs, ou
         offsets = keep.tile([P, N // 16], U16, name="offsets")
         nc.sync.dma_start(offsets[:], offs)
         scale_pool = keep.tile([P, T], U8, name="scale_pool", align_bytes=64)
-        nc.scalar.dma_start(scale_pool[96:P, :].bitcast(I32), k_scales.bitcast(I32).rearrange("o f t -> f o t"))
+        nc.sync.dma_start(scale_pool[96:P, :].bitcast(I32), k_scales.bitcast(I32).rearrange("o f t -> f o t"))
         age_pool = keep.tile([P, T], F32, name="age_pool", align_bytes=64)
         nc.sync.dma_start(age_pool[AGE_ROW:P, :], ag[0:1, :])
         word_pool = shared.tile([P, T], I32, name="word_pool", offset=0, align_bytes=64)
-        nc.sync.dma_start(word_pool[:], k_words[0].rearrange("p t b -> p (t b)").bitcast(I32))
         q_raw = [keep.tile([P, PACK, NQ], F32, name=f"q_raw{o}") for o in range(PASSES)]
         q_rows = qT[0].rearrange("(o p j) n -> o p j n", o=PASSES, j=PACK)
-        for o in range(PASSES):
-            nc.sync.dma_start(q_raw[o][:], q_rows[o])
+        nc.sync.dma_start(q_raw[0][:], q_rows[0])
+        nc.sync.dma_start(word_pool[:], k_words[0].rearrange("p t b -> p (t b)").bitcast(I32))
+        nc.sync.dma_start(q_raw[1][:], q_rows[1])
         rate = keep.tile([P, 1], F32, name="rate")
         nc.sync.dma_start(rate[:], rt[0])
 
@@ -67,7 +67,7 @@ def tile_attend_link_age_topk_kernel(tc, qT, k_words, k_scales, ag, rt, offs, ou
                 scale_rows[96 + 8 * quad : 96 + 8 * (quad + 1), :].bitcast(I32),
             )
 
-        ages0 = shared.tile([P, N // 2], F32, name="ages0", offset=4 * T + 1024, align_bytes=64)
+        ages0 = keep.tile([P, N // 2], F32, name="ages0")
         ages1 = shared.tile([P, N // 2], F32, name="ages1", offset=4 * T, align_bytes=64)
         ages = [ages0, ages1]
         turned = [psum.tile([P, 2, P], F32, name=f"turned{h}") for h in range(2)]
@@ -77,7 +77,7 @@ def tile_attend_link_age_topk_kernel(tc, qT, k_words, k_scales, ag, rt, offs, ou
                 nc.tensor.transpose(turned[h][:, c, :], ages[h][:, c * P : (c + 1) * P], ident[:])
 
         spread = psum.tile([P, 4, P], F32, name="spread")
-        q_bf0 = shared.tile([P, NQ, PACK], BF16, name="q_bf0", offset=4 * T + 1024, align_bytes=64)
+        q_bf0 = keep.tile([P, NQ, PACK], BF16, name="q_bf0", align_bytes=64)
         q_bf1 = shared.tile([P, NQ, PACK], BF16, name="q_bf1", offset=4 * T, align_bytes=64)
         q_bf = [q_bf0, q_bf1]
         for h in range(2):
@@ -91,7 +91,7 @@ def tile_attend_link_age_topk_kernel(tc, qT, k_words, k_scales, ag, rt, offs, ou
                 ACT.Copy,
             )
 
-        q_codes0 = shared.tile([P, NQ], U32, name="q_codes0", offset=512, align_bytes=64)
+        q_codes0 = keep.tile([P, NQ], U32, name="q_codes0", align_bytes=64)
         q_codes1 = shared.tile([P, NQ], U32, name="q_codes1", offset=4 * T + 2048, align_bytes=64)
         q_codes = [q_codes0, q_codes1]
         q_planes = [keep.tile([P, NQ], U8, name=f"q_plane{o}", align_bytes=64) for o in range(PASSES)]
@@ -135,16 +135,12 @@ def tile_attend_link_age_topk_kernel(tc, qT, k_words, k_scales, ag, rt, offs, ou
                 stop=(o == PASSES - 1),
             )
 
-        res_first = keep.tile([P, 2 * P], F32, name="res_first")
-        res_last = [keep.tile([P, P], F32, name=f"res_last{c}") for c in range(2)]
-        res = [res_first[:, 0:P], res_first[:, P : 2 * P], res_last[0][:], res_last[1][:]]
+        res = [keep.tile([P, 2, P], F32, name=f"res{h}") for h in range(2)]
         for c in range(4):
             th = keep.tile([P, P], F32, name=f"th{c}")
             nc.scalar.activation(th[:], scores[c][:], ACT.Tanh, scale=0.5)
             nc.vector.scalar_tensor_tensor(
-                res[c], th[:], 1.0, half_decay[:, P * c : P * (c + 1)], ALU.add, ALU.mult
+                res[c // 2][:, c % 2, :], th[:], 1.0, half_decay[:, P * c : P * (c + 1)], ALU.add, ALU.mult
             )
-            if c == 1:
-                nc.sync.dma_start(out[0, :, 0 : 2 * P], res_first[:])
-            elif c > 1:
-                nc.sync.dma_start(out[0, :, P * c : P * (c + 1)], res[c])
+            if c % 2 == 1:
+                nc.sync.dma_start(out[0, :, P * (c - 1) : P * (c + 1)], res[c // 2][:].rearrange("p a n -> p (a n)"))

@@ -98,9 +98,7 @@ def tile_attend_link_age_topk_kernel(tc, qT, k_words, k_scales, ag, rt, offs, ou
         words0 = shared.tile([P, N // 2], U32, name="words0", offset=4 * T + 2048, align_bytes=64)
         words1 = keep.tile([P, N // 2], U32, name="words1", align_bytes=64)
         words = [words0, words1]
-        k_first = [keep.tile([P, PASSES, 2 * P], U8, name=f"k_first{c}", align_bytes=64) for c in range(2)]
-        k_last = keep.tile([P, PASSES, N], U8, name="k_last", align_bytes=64)
-        k_codes = [k_first[0][:], k_first[1][:], k_last[:, :, 0 : 2 * P], k_last[:, :, 2 * P : N]]
+        k_codes = [keep.tile([P, PASSES, 2 * P], U8, name=f"k_codes{c}", align_bytes=64) for c in range(4)]
 
         def quantize(o):
             nc.vector.quantize_mx(
@@ -112,11 +110,11 @@ def tile_attend_link_age_topk_kernel(tc, qT, k_words, k_scales, ag, rt, offs, ou
 
         for h in range(2):
             nc.vector.tensor_copy(words[h][:], word_pool[:].bitcast(U32).indirect(offsets[:, 16 * h : 16 * (h + 1)]))
-        split(k_first[0][:], words0[:, 0:P])
         quantize(0)
-        split(k_first[1][:], words0[:, P : 2 * P])
-        split(k_last[:], words1[:])
-        quantize(1)
+        for c in range(4):
+            if c == 3:
+                quantize(1)
+            split(k_codes[c][:], words[c // 2][:, P * (c % 2) : P * (c % 2 + 1)])
 
         half_decay = keep.tile([P, N], F32, name="half_decay")
         nc.scalar.activation(
@@ -124,7 +122,7 @@ def tile_attend_link_age_topk_kernel(tc, qT, k_words, k_scales, ag, rt, offs, ou
         )
 
         scores = [psum.tile([P, P], F32, name=f"scores{c}") for c in range(4)]
-        for c, o in [(c, o) for o in range(PASSES) for c in range(4)]:
+        for c, o in [(c, o) for o in range(PASSES) for c in range(3)] + [(3, o) for o in range(PASSES)]:
             nc.tensor.matmul_mx(
                 out=scores[c][:],
                 lhsT=q_codes[o][:].bitcast(FP8X4),

@@ -31,6 +31,7 @@ def tile_attend_link_age_topk_kernel(tc, qT, k_words, k_scales, ag, rt, offs, ou
     with ExitStack() as ctx:
         keep = ctx.enter_context(tc.tile_pool(name="keep", bufs=1))
         shared = ctx.enter_context(tc.tile_pool(name="shared", bufs=1))
+        late = ctx.enter_context(tc.tile_pool(name="late", bufs=1))
         psum = ctx.enter_context(tc.psum_pool(name="psum", bufs=1))
 
         offsets = keep.tile([P, N // 16], U16, name="offsets")
@@ -40,7 +41,9 @@ def tile_attend_link_age_topk_kernel(tc, qT, k_words, k_scales, ag, rt, offs, ou
         age_pool = keep.tile([P, T], F32, name="age_pool", align_bytes=64)
         nc.sync.dma_start(age_pool[AGE_ROW:P, :], ag[0:1, :])
         word_pool = shared.tile([P, T], I32, name="word_pool", offset=0, align_bytes=64)
-        q_raw = [keep.tile([P, PACK, NQ], F32, name=f"q_raw{o}") for o in range(PASSES)]
+        q_raw0 = keep.tile([P, PACK, NQ], F32, name="q_raw0")
+        q_raw1 = late.tile([P, PACK, NQ], F32, name="q_raw1", offset=0, align_bytes=64)
+        q_raw = [q_raw0, q_raw1]
         q_rows = qT[0].rearrange("(o p j) n -> o p j n", o=PASSES, j=PACK)
         nc.sync.dma_start(q_raw[0][:], q_rows[0])
         nc.sync.dma_start(word_pool[:], k_words[0].rearrange("p t b -> p (t b)").bitcast(I32))
@@ -55,9 +58,9 @@ def tile_attend_link_age_topk_kernel(tc, qT, k_words, k_scales, ag, rt, offs, ou
         for region, lo, mid, hi in ((scale_words, 0, 255, 512), (age_words, 0, 511, AGE_SPLIT), (plane_words, 0, 127, 256)):
             nc.vector.memset(region[:, lo:mid], 0)
             nc.vector.memset(region[:, mid:hi], 0)
-        nc.gpsimd.memset(age_words[:, AGE_SPLIT:T], 0)
         ident = keep.tile([P, P], F32, name="ident")
         make_identity(nc, ident[:])
+        nc.gpsimd.memset(age_words[:, AGE_SPLIT:T], 0)
 
         scale_rows = keep.tile([P, N], U8, name="scale_rows", align_bytes=64)
         nc.vector.tensor_copy(scale_rows[:], scale_pool[:].indirect(offsets[:]))
@@ -92,13 +95,16 @@ def tile_attend_link_age_topk_kernel(tc, qT, k_words, k_scales, ag, rt, offs, ou
             )
 
         q_codes0 = keep.tile([P, NQ], U32, name="q_codes0", align_bytes=64)
-        q_codes1 = shared.tile([P, NQ], U32, name="q_codes1", offset=4 * T + 2048, align_bytes=64)
+        q_codes1 = keep.tile([P, NQ], U32, name="q_codes1", align_bytes=64)
         q_codes = [q_codes0, q_codes1]
         q_planes = [keep.tile([P, NQ], U8, name=f"q_plane{o}", align_bytes=64) for o in range(PASSES)]
         words0 = shared.tile([P, N // 2], U32, name="words0", offset=4 * T + 2048, align_bytes=64)
         words1 = keep.tile([P, N // 2], U32, name="words1", align_bytes=64)
         words = [words0, words1]
-        k_codes = [keep.tile([P, PASSES, 2 * P], U8, name=f"k_codes{c}", align_bytes=64) for c in range(4)]
+        k_codes = [keep.tile([P, PASSES, 2 * P], U8, name=f"k_codes{c}", align_bytes=64) for c in range(2)]
+        k_codes = k_codes + [
+            late.tile([P, PASSES, 2 * P], U8, name=f"k_codes{c}", offset=512 * (c - 2), align_bytes=64) for c in range(2, 4)
+        ]
 
         def quantize(o):
             nc.vector.quantize_mx(
@@ -112,7 +118,7 @@ def tile_attend_link_age_topk_kernel(tc, qT, k_words, k_scales, ag, rt, offs, ou
             nc.vector.tensor_copy(words[h][:], word_pool[:].bitcast(U32).indirect(offsets[:, 16 * h : 16 * (h + 1)]))
         quantize(0)
         for c in range(4):
-            if c == 3:
+            if c == 2:
                 quantize(1)
             split(k_codes[c][:], words[c // 2][:, P * (c % 2) : P * (c % 2 + 1)])
 
@@ -122,7 +128,7 @@ def tile_attend_link_age_topk_kernel(tc, qT, k_words, k_scales, ag, rt, offs, ou
         )
 
         scores = [psum.tile([P, P], F32, name=f"scores{c}") for c in range(4)]
-        for c, o in [(c, o) for o in range(PASSES) for c in range(3)] + [(3, o) for o in range(PASSES)]:
+        for c, o in [(c, o) for o in range(PASSES) for c in range(2)] + [(c, o) for c in range(2, 4) for o in range(PASSES)]:
             nc.tensor.matmul_mx(
                 out=scores[c][:],
                 lhsT=q_codes[o][:].bitcast(FP8X4),
@@ -134,11 +140,15 @@ def tile_attend_link_age_topk_kernel(tc, qT, k_words, k_scales, ag, rt, offs, ou
             )
 
         res = [keep.tile([P, 2, P], F32, name=f"res{h}") for h in range(2)]
-        for c in range(4):
-            th = keep.tile([P, P], F32, name=f"th{c}")
-            nc.scalar.activation(th[:], scores[c][:], ACT.Tanh, scale=0.5)
+        pieces = [(0, P), (P, 2 * P), (2 * P, 3 * P), (3 * P, 3 * P + P // 2), (3 * P + P // 2, N)]
+        for lo, hi in pieces:
+            c = lo // P
+            th = keep.tile([P, hi - lo], F32, name=f"th{lo}")
+            nc.scalar.activation(th[:], scores[c][:, lo - c * P : hi - c * P], ACT.Tanh, scale=0.5)
+            half = lo // (2 * P)
+            flat = res[half][:].rearrange("p a n -> p (a n)")
             nc.vector.scalar_tensor_tensor(
-                res[c // 2][:, c % 2, :], th[:], 1.0, half_decay[:, P * c : P * (c + 1)], ALU.add, ALU.mult
+                flat[:, lo - half * 2 * P : hi - half * 2 * P], th[:], 1.0, half_decay[:, lo:hi], ALU.add, ALU.mult
             )
-            if c % 2 == 1:
-                nc.sync.dma_start(out[0, :, P * (c - 1) : P * (c + 1)], res[c // 2][:].rearrange("p a n -> p (a n)"))
+            if hi % (2 * P) == 0:
+                nc.sync.dma_start(out[0, :, hi - 2 * P : hi], flat)

@@ -34,10 +34,10 @@ def tile_attend_link_age_topk_kernel(tc, qT, k_words, k_scales, ag, rt, offs, ou
         late = ctx.enter_context(tc.tile_pool(name="late", bufs=1))
         psum = ctx.enter_context(tc.psum_pool(name="psum", bufs=1))
 
-        offsets = keep.tile([P, N // 16], U16, name="offsets")
-        nc.sync.dma_start(offsets[:], offs)
         scale_pool = keep.tile([P, T], U8, name="scale_pool", align_bytes=64)
         nc.sync.dma_start(scale_pool[96:P, :].bitcast(I32), k_scales.bitcast(I32).rearrange("o f t -> f o t"))
+        offsets = keep.tile([P, N // 16], U16, name="offsets")
+        nc.sync.dma_start(offsets[:], offs)
         age_pool = keep.tile([P, T], F32, name="age_pool", align_bytes=64)
         nc.sync.dma_start(age_pool[AGE_ROW:P, :], ag[0:1, :])
         word_pool = shared.tile([P, T], I32, name="word_pool", offset=0, align_bytes=64)
@@ -73,24 +73,27 @@ def tile_attend_link_age_topk_kernel(tc, qT, k_words, k_scales, ag, rt, offs, ou
         ages0 = keep.tile([P, N // 2], F32, name="ages0")
         ages1 = shared.tile([P, N // 2], F32, name="ages1", offset=4 * T, align_bytes=64)
         ages = [ages0, ages1]
-        turned = [psum.tile([P, 2, P], F32, name=f"turned{h}") for h in range(2)]
+        groups = [(0, 1), (2,), (3,)]
+        turned = [psum.tile([P, len(group), P], F32, name=f"turned{g}") for g, group in enumerate(groups)]
+        place = {c: turned[g][:, i, :] for g, group in enumerate(groups) for i, c in enumerate(group)}
         for h in range(2):
             nc.vector.tensor_copy(ages[h][:], age_pool[:].indirect(offsets[:, 16 * h : 16 * (h + 1)]))
             for c in range(2):
-                nc.tensor.transpose(turned[h][:, c, :], ages[h][:, c * P : (c + 1) * P], ident[:])
+                nc.tensor.transpose(place[2 * h + c], ages[h][:, c * P : (c + 1) * P], ident[:])
 
         spread = psum.tile([P, 4, P], F32, name="spread")
         q_bf0 = keep.tile([P, NQ, PACK], BF16, name="q_bf0", align_bytes=64)
         q_bf1 = shared.tile([P, NQ, PACK], BF16, name="q_bf1", offset=4 * T, align_bytes=64)
         q_bf = [q_bf0, q_bf1]
-        for h in range(2):
-            age_cols = keep.tile([P, 2], F32, name=f"age_cols{h}")
-            nc.scalar.activation(age_cols[:], turned[h][:, :, AGE_ROW], ACT.Copy, scale=-1.0)
-            for c in range(2):
-                nc.tensor.transpose(spread[:, 2 * h + c, :], age_cols[:, c : c + 1].to_broadcast([P, P]), ident[:])
+        for g, group in enumerate(groups):
+            age_cols = keep.tile([P, len(group)], F32, name=f"age_cols{g}")
+            nc.scalar.activation(age_cols[:], turned[g][:, :, AGE_ROW], ACT.Copy, scale=-1.0)
+            for i, c in enumerate(group):
+                nc.tensor.transpose(spread[:, c, :], age_cols[:, i : i + 1].to_broadcast([P, P]), ident[:])
+        for o in range(PASSES):
             nc.scalar.activation(
-                q_bf[h][:].rearrange("p (c i) j -> p c j i", i=4),
-                q_raw[h][:].rearrange("p j (c i) -> p c j i", i=4),
+                q_bf[o][:].rearrange("p (c i) j -> p c j i", i=4),
+                q_raw[o][:].rearrange("p j (c i) -> p c j i", i=4),
                 ACT.Copy,
             )
 
@@ -101,26 +104,41 @@ def tile_attend_link_age_topk_kernel(tc, qT, k_words, k_scales, ag, rt, offs, ou
         words0 = shared.tile([P, N // 2], U32, name="words0", offset=4 * T + 2048, align_bytes=64)
         words1 = keep.tile([P, N // 2], U32, name="words1", align_bytes=64)
         words = [words0, words1]
-        k_codes = [keep.tile([P, PASSES, 2 * P], U8, name=f"k_codes{c}", align_bytes=64) for c in range(2)]
-        k_codes = k_codes + [
-            late.tile([P, PASSES, 2 * P], U8, name=f"k_codes{c}", offset=512 * (c - 2), align_bytes=64) for c in range(2, 4)
-        ]
+        ahead = [(0, 0), (1, 0), (0, 1), (2, 0)]
+        behind = [(1, 1), (2, 1)]
+        parts = {part: keep.tile([P, 2 * P], U8, name=f"codes{part[0]}{part[1]}", align_bytes=64) for part in ahead}
+        late_parts = {
+            part: late.tile([P, 2 * P], U8, name=f"codes{part[0]}{part[1]}", offset=2 * P * i, align_bytes=64)
+            for i, part in enumerate(behind)
+        }
+        last = late.tile([P, PASSES, 2 * P], U8, name="codes3", offset=4 * P, align_bytes=64)
 
         def quantize(o):
             nc.vector.quantize_mx(
                 out=q_codes[o][:].bitcast(FP8X4), scales=q_planes[o][:], in_=q_bf[o][:].rearrange("p n j -> p (n j)")
             )
 
-        def split(dst, src):
-            nc.vector.tensor_copy(dst.bitcast(U16), src.bitcast(U16).rearrange("p (n o) -> p o n", o=PASSES))
+        def halves_of(src):
+            return src.bitcast(U16).rearrange("p (n o) -> p o n", o=PASSES)
 
         for h in range(2):
             nc.vector.tensor_copy(words[h][:], word_pool[:].bitcast(U32).indirect(offsets[:, 16 * h : 16 * (h + 1)]))
         quantize(0)
-        for c in range(4):
-            if c == 2:
-                quantize(1)
-            split(k_codes[c][:], words[c // 2][:, P * (c % 2) : P * (c % 2 + 1)])
+
+        def block_words(c):
+            return halves_of(words[c // 2][:, P * (c % 2) : P * (c % 2 + 1)])
+
+        for c, o in ahead:
+            nc.vector.tensor_copy(parts[(c, o)][:].bitcast(U16), block_words(c)[:, o, :])
+        quantize(1)
+        for c, o in behind:
+            nc.vector.tensor_copy(late_parts[(c, o)][:].bitcast(U16), block_words(c)[:, o, :])
+        nc.vector.tensor_copy(last[:].bitcast(U16), block_words(3))
+        k_codes = dict(
+            [(part, parts[part][:]) for part in ahead]
+            + [(part, late_parts[part][:]) for part in behind]
+            + [((3, o), last[:, o, :]) for o in range(PASSES)]
+        )
 
         half_decay = keep.tile([P, N], F32, name="half_decay")
         nc.scalar.activation(
@@ -128,12 +146,12 @@ def tile_attend_link_age_topk_kernel(tc, qT, k_words, k_scales, ag, rt, offs, ou
         )
 
         scores = [psum.tile([P, P], F32, name=f"scores{c}") for c in range(4)]
-        for c, o in [(c, o) for o in range(PASSES) for c in range(2)] + [(c, o) for c in range(2, 4) for o in range(PASSES)]:
+        for c, o in [(c, o) for o in range(PASSES) for c in range(3)] + [(3, o) for o in range(PASSES)]:
             nc.tensor.matmul_mx(
                 out=scores[c][:],
                 lhsT=q_codes[o][:].bitcast(FP8X4),
                 lhsT_scale=q_planes[o][:],
-                rhs=k_codes[c][:, o, :].bitcast(FP4X4),
+                rhs=k_codes[(c, o)].bitcast(FP4X4),
                 rhs_scale=k_planes[:, o * N + P * c : o * N + P * (c + 1)],
                 start=(o == 0),
                 stop=(o == PASSES - 1),

@@ -31,7 +31,6 @@ def tile_attend_link_age_topk_kernel(tc, qT, k_words, k_scales, ag, rt, offs, ou
     with ExitStack() as ctx:
         keep = ctx.enter_context(tc.tile_pool(name="keep", bufs=1))
         shared = ctx.enter_context(tc.tile_pool(name="shared", bufs=1))
-        late = ctx.enter_context(tc.tile_pool(name="late", bufs=1))
         psum = ctx.enter_context(tc.psum_pool(name="psum", bufs=1))
 
         scale_pool = keep.tile([P, T], U8, name="scale_pool", align_bytes=64)
@@ -41,26 +40,29 @@ def tile_attend_link_age_topk_kernel(tc, qT, k_words, k_scales, ag, rt, offs, ou
         age_pool = keep.tile([P, T], F32, name="age_pool", align_bytes=64)
         nc.sync.dma_start(age_pool[AGE_ROW:P, :], ag[0:1, :])
         word_pool = shared.tile([P, T], I32, name="word_pool", offset=0, align_bytes=64)
-        q_raw0 = keep.tile([P, PACK, NQ], F32, name="q_raw0")
-        q_raw1 = late.tile([P, PACK, NQ], F32, name="q_raw1", offset=0, align_bytes=64)
-        q_raw = [q_raw0, q_raw1]
-        q_rows = qT[0].rearrange("(o p j) n -> o p j n", o=PASSES, j=PACK)
-        nc.sync.dma_start(q_raw[0][:], q_rows[0])
         nc.sync.dma_start(word_pool[:], k_words[0].rearrange("p t b -> p (t b)").bitcast(I32))
-        nc.sync.dma_start(q_raw[1][:], q_rows[1])
+        q_raw = [keep.tile([P, PACK, NQ], F32, name=f"q_raw{o}") for o in range(PASSES)]
+        q_rows = qT[0].rearrange("(o p j) n -> o p j n", o=PASSES, j=PACK)
+        for o in range(PASSES):
+            nc.sync.dma_start(q_raw[o][:], q_rows[o])
         rate = keep.tile([P, 1], F32, name="rate")
         nc.sync.dma_start(rate[:], rt[0])
 
-        k_planes = keep.tile([P, PASSES * N], U8, name="k_planes", align_bytes=64)
+        one = keep.tile([P, 1], F32, name="one")
+        nc.vector.memset(one[:], 1.0)
+        log_half = keep.tile([P, 1], F32, name="log_half")
+        nc.scalar.activation(log_half[:], one[:], ACT.Copy, scale=-math.log(2.0))
+
         scale_words = scale_pool[0:96, :].bitcast(I32)
         age_words = age_pool[0:AGE_ROW, :].bitcast(I32)
-        plane_words = k_planes[:].bitcast(I32)
-        for region, lo, mid, hi in ((scale_words, 0, 255, 512), (age_words, 0, 511, AGE_SPLIT), (plane_words, 0, 127, 256)):
+        for region, lo, mid, hi in ((scale_words, 0, 255, 512), (age_words, 0, 511, AGE_SPLIT)):
             nc.vector.memset(region[:, lo:mid], 0)
             nc.vector.memset(region[:, mid:hi], 0)
+        nc.gpsimd.memset(age_words[:, AGE_SPLIT:T], 0)
         ident = keep.tile([P, P], F32, name="ident")
         make_identity(nc, ident[:])
-        nc.gpsimd.memset(age_words[:, AGE_SPLIT:T], 0)
+        k_planes = keep.tile([P, PASSES * N], U8, name="k_planes", align_bytes=64)
+        nc.gpsimd.memset(k_planes[:].bitcast(I32), 0)
 
         scale_rows = keep.tile([P, N], U8, name="scale_rows", align_bytes=64)
         nc.vector.tensor_copy(scale_rows[:], scale_pool[:].indirect(offsets[:]))
@@ -71,25 +73,25 @@ def tile_attend_link_age_topk_kernel(tc, qT, k_words, k_scales, ag, rt, offs, ou
             )
 
         ages0 = keep.tile([P, N // 2], F32, name="ages0")
-        ages1 = shared.tile([P, N // 2], F32, name="ages1", offset=4 * T, align_bytes=64)
+        ages1 = shared.tile([P, N // 2], F32, name="ages1", offset=4 * T + 512, align_bytes=64)
         ages = [ages0, ages1]
-        groups = [(0, 1), (2,), (3,)]
-        turned = [psum.tile([P, len(group), P], F32, name=f"turned{g}") for g, group in enumerate(groups)]
-        place = {c: turned[g][:, i, :] for g, group in enumerate(groups) for i, c in enumerate(group)}
-        for h in range(2):
-            nc.vector.tensor_copy(ages[h][:], age_pool[:].indirect(offsets[:, 16 * h : 16 * (h + 1)]))
-            for c in range(2):
-                nc.tensor.transpose(place[2 * h + c], ages[h][:, c * P : (c + 1) * P], ident[:])
-
+        turned = [psum.tile([P, 2, P], F32, name=f"turned{h}") for h in range(2)]
         spread = psum.tile([P, 4, P], F32, name="spread")
-        q_bf0 = keep.tile([P, NQ, PACK], BF16, name="q_bf0", align_bytes=64)
-        q_bf1 = shared.tile([P, NQ, PACK], BF16, name="q_bf1", offset=4 * T, align_bytes=64)
-        q_bf = [q_bf0, q_bf1]
-        for g, group in enumerate(groups):
-            age_cols = keep.tile([P, len(group)], F32, name=f"age_cols{g}")
-            nc.scalar.activation(age_cols[:], turned[g][:, :, AGE_ROW], ACT.Copy, scale=-1.0)
-            for i, c in enumerate(group):
-                nc.tensor.transpose(spread[:, c, :], age_cols[:, i : i + 1].to_broadcast([P, P]), ident[:])
+        for h in range(2):
+            nc.scalar.activation(ages[h][:], age_pool[:].indirect(offsets[:, 16 * h : 16 * (h + 1)]), ACT.Copy)
+        for h in range(2):
+            for c in range(2):
+                nc.tensor.transpose(turned[h][:, c, :], ages[h][:, c * P : (c + 1) * P], ident[:])
+        for h in range(2):
+            age_cols = keep.tile([P, 2], F32, name=f"age_cols{h}")
+            nc.scalar.activation(age_cols[:], turned[h][:, :, AGE_ROW], ACT.Copy, scale=-1.0)
+            for c in range(2):
+                nc.tensor.transpose(spread[:, 2 * h + c, :], age_cols[:, c : c + 1].to_broadcast([P, P]), ident[:])
+
+        q_bf = [
+            shared.tile([P, NQ, PACK], BF16, name=f"q_bf{o}", offset=4 * T + 1024 * o, align_bytes=64)
+            for o in range(PASSES)
+        ]
         for o in range(PASSES):
             nc.scalar.activation(
                 q_bf[o][:].rearrange("p (c i) j -> p c j i", i=4),
@@ -97,65 +99,51 @@ def tile_attend_link_age_topk_kernel(tc, qT, k_words, k_scales, ag, rt, offs, ou
                 ACT.Copy,
             )
 
-        q_codes0 = keep.tile([P, NQ], U32, name="q_codes0", align_bytes=64)
-        q_codes1 = keep.tile([P, NQ], U32, name="q_codes1", align_bytes=64)
-        q_codes = [q_codes0, q_codes1]
+        words = [keep.tile([P, N // 2], U32, name=f"words{h}", align_bytes=64) for h in range(2)]
+        for h in range(2):
+            nc.vector.tensor_copy(words[h][:], word_pool[:].bitcast(U32).indirect(offsets[:, 16 * h : 16 * (h + 1)]))
+
+        q_codes = [shared.tile([P, NQ], U32, name=f"q_codes{o}", offset=512 * o, align_bytes=64) for o in range(PASSES)]
         q_planes = [keep.tile([P, NQ], U8, name=f"q_plane{o}", align_bytes=64) for o in range(PASSES)]
-        words0 = shared.tile([P, N // 2], U32, name="words0", offset=4 * T + 2048, align_bytes=64)
-        words1 = keep.tile([P, N // 2], U32, name="words1", align_bytes=64)
-        words = [words0, words1]
-        ahead = [(0, 0), (1, 0), (0, 1), (2, 0)]
-        behind = [(1, 1), (2, 1)]
-        parts = {part: keep.tile([P, 2 * P], U8, name=f"codes{part[0]}{part[1]}", align_bytes=64) for part in ahead}
-        late_parts = {
-            part: late.tile([P, 2 * P], U8, name=f"codes{part[0]}{part[1]}", offset=2 * P * i, align_bytes=64)
-            for i, part in enumerate(behind)
-        }
-        last = late.tile([P, PASSES, 2 * P], U8, name="codes3", offset=4 * P, align_bytes=64)
+        k_codes = {}
 
         def quantize(o):
             nc.vector.quantize_mx(
                 out=q_codes[o][:].bitcast(FP8X4), scales=q_planes[o][:], in_=q_bf[o][:].rearrange("p n j -> p (n j)")
             )
 
-        def halves_of(src):
-            return src.bitcast(U16).rearrange("p (n o) -> p o n", o=PASSES)
+        def part(o, first, count):
+            codes = keep.tile([P, count * 2 * P], U8, name=f"codes{o}{first}", align_bytes=64)
+            src = words[first // 2][:, P * (first % 2) : P * (first % 2 + count)]
+            nc.vector.tensor_copy(codes[:].bitcast(U16), src.bitcast(U16).rearrange("p (n o) -> p o n", o=PASSES)[:, o, :])
+            for i in range(count):
+                k_codes[(first + i, o)] = codes[:, 2 * P * i : 2 * P * (i + 1)]
 
-        for h in range(2):
-            nc.vector.tensor_copy(words[h][:], word_pool[:].bitcast(U32).indirect(offsets[:, 16 * h : 16 * (h + 1)]))
+        part(0, 0, 2)
         quantize(0)
-
-        def block_words(c):
-            return halves_of(words[c // 2][:, P * (c % 2) : P * (c % 2 + 1)])
-
-        for c, o in ahead:
-            nc.vector.tensor_copy(parts[(c, o)][:].bitcast(U16), block_words(c)[:, o, :])
+        part(0, 2, 2)
+        part(1, 0, 2)
         quantize(1)
-        for c, o in behind:
-            nc.vector.tensor_copy(late_parts[(c, o)][:].bitcast(U16), block_words(c)[:, o, :])
-        nc.vector.tensor_copy(last[:].bitcast(U16), block_words(3))
-        k_codes = dict(
-            [(part, parts[part][:]) for part in ahead]
-            + [(part, late_parts[part][:]) for part in behind]
-            + [((3, o), last[:, o, :]) for o in range(PASSES)]
-        )
+        part(1, 2, 1)
+        part(1, 3, 1)
 
         half_decay = keep.tile([P, N], F32, name="half_decay")
         nc.scalar.activation(
-            half_decay[:], spread[:].rearrange("p c n -> p (c n)"), ACT.Exp, scale=rate[:, 0:1], bias=-math.log(2.0)
+            half_decay[:], spread[:].rearrange("p c n -> p (c n)"), ACT.Exp, scale=rate[:, 0:1], bias=log_half[:, 0:1]
         )
 
         scores = [psum.tile([P, P], F32, name=f"scores{c}") for c in range(4)]
-        for c, o in [(c, o) for o in range(PASSES) for c in range(3)] + [(3, o) for o in range(PASSES)]:
-            nc.tensor.matmul_mx(
-                out=scores[c][:],
-                lhsT=q_codes[o][:].bitcast(FP8X4),
-                lhsT_scale=q_planes[o][:],
-                rhs=k_codes[(c, o)].bitcast(FP4X4),
-                rhs_scale=k_planes[:, o * N + P * c : o * N + P * (c + 1)],
-                start=(o == 0),
-                stop=(o == PASSES - 1),
-            )
+        for o in range(PASSES):
+            for c in range(4):
+                nc.tensor.matmul_mx(
+                    out=scores[c][:],
+                    lhsT=q_codes[o][:].bitcast(FP8X4),
+                    lhsT_scale=q_planes[o][:],
+                    rhs=k_codes[(c, o)].bitcast(FP4X4),
+                    rhs_scale=k_planes[:, o * N + P * c : o * N + P * (c + 1)],
+                    start=(o == 0),
+                    stop=(o == PASSES - 1),
+                )
 
         res = [keep.tile([P, 2, P], F32, name=f"res{h}") for h in range(2)]
         pieces = [(0, P), (P, 2 * P), (2 * P, 3 * P), (3 * P, 3 * P + P // 2), (3 * P + P // 2, N)]

@@ -31,13 +31,14 @@ def tile_attend_link_age_topk_kernel(tc, qT, k_words, k_scales, ag, rt, offs, ou
     with ExitStack() as ctx:
         keep = ctx.enter_context(tc.tile_pool(name="keep", bufs=1))
         shared = ctx.enter_context(tc.tile_pool(name="shared", bufs=1))
+        aged = ctx.enter_context(tc.tile_pool(name="aged", bufs=1))
         psum = ctx.enter_context(tc.psum_pool(name="psum", bufs=1))
 
         scale_pool = keep.tile([P, T], U8, name="scale_pool", align_bytes=64)
         nc.sync.dma_start(scale_pool[96:P, :].bitcast(I32), k_scales.bitcast(I32).rearrange("o f t -> f o t"))
         offsets = keep.tile([P, N // 16], U16, name="offsets")
         nc.sync.dma_start(offsets[:], offs)
-        age_pool = keep.tile([P, T], F32, name="age_pool", align_bytes=64)
+        age_pool = aged.tile([P, T], F32, name="age_pool", offset=0, align_bytes=64)
         nc.sync.dma_start(age_pool[AGE_ROW:P, :], ag[0:1, :])
         word_pool = shared.tile([P, T], I32, name="word_pool", offset=0, align_bytes=64)
         nc.sync.dma_start(word_pool[:], k_words[0].rearrange("p t b -> p (t b)").bitcast(I32))
@@ -61,16 +62,9 @@ def tile_attend_link_age_topk_kernel(tc, qT, k_words, k_scales, ag, rt, offs, ou
         nc.gpsimd.memset(age_words[:, AGE_SPLIT:T], 0)
         ident = keep.tile([P, P], F32, name="ident")
         make_identity(nc, ident[:])
-        k_planes = keep.tile([P, PASSES * N], U8, name="k_planes", align_bytes=64)
-        nc.gpsimd.memset(k_planes[:].bitcast(I32), 0)
 
         scale_rows = keep.tile([P, N], U8, name="scale_rows", align_bytes=64)
         nc.vector.tensor_copy(scale_rows[:], scale_pool[:].indirect(offsets[:]))
-        for quad in range(4):
-            nc.sync.dma_start(
-                k_planes[32 * quad : 32 * quad + 4, :].bitcast(I32),
-                scale_rows[96 + 8 * quad : 96 + 8 * (quad + 1), :].bitcast(I32),
-            )
 
         ages0 = keep.tile([P, N // 2], F32, name="ages0")
         ages1 = shared.tile([P, N // 2], F32, name="ages1", offset=4 * T + 512, align_bytes=64)
@@ -79,6 +73,12 @@ def tile_attend_link_age_topk_kernel(tc, qT, k_words, k_scales, ag, rt, offs, ou
         spread = psum.tile([P, 4, P], F32, name="spread")
         for h in range(2):
             nc.scalar.activation(ages[h][:], age_pool[:].indirect(offsets[:, 16 * h : 16 * (h + 1)]), ACT.Copy)
+        k_planes = aged.tile([P, PASSES * N], U8, name="k_planes", offset=0, align_bytes=64)
+        for quad in range(4):
+            nc.scalar.dma_start(
+                k_planes[32 * quad : 32 * quad + 4, :].bitcast(I32),
+                scale_rows[96 + 8 * quad : 96 + 8 * (quad + 1), :].bitcast(I32),
+            )
         for h in range(2):
             for c in range(2):
                 nc.tensor.transpose(turned[h][:, c, :], ages[h][:, c * P : (c + 1) * P], ident[:])

@@ -31,14 +31,14 @@ def tile_attend_link_age_topk_kernel(tc, qT, k_words, k_scales, ag, rt, offs, ou
     with ExitStack() as ctx:
         keep = ctx.enter_context(tc.tile_pool(name="keep", bufs=1))
         shared = ctx.enter_context(tc.tile_pool(name="shared", bufs=1))
-        aged = ctx.enter_context(tc.tile_pool(name="aged", bufs=1))
+        scaled = ctx.enter_context(tc.tile_pool(name="scaled", bufs=1))
         psum = ctx.enter_context(tc.psum_pool(name="psum", bufs=1))
 
-        scale_pool = keep.tile([P, T], U8, name="scale_pool", align_bytes=64)
+        scale_pool = scaled.tile([P, T], U8, name="scale_pool", offset=0, align_bytes=64)
         nc.sync.dma_start(scale_pool[96:P, :].bitcast(I32), k_scales.bitcast(I32).rearrange("o f t -> f o t"))
         offsets = keep.tile([P, N // 16], U16, name="offsets")
         nc.sync.dma_start(offsets[:], offs)
-        age_pool = aged.tile([P, T], F32, name="age_pool", offset=0, align_bytes=64)
+        age_pool = keep.tile([P, T], F32, name="age_pool", align_bytes=64)
         nc.sync.dma_start(age_pool[AGE_ROW:P, :], ag[0:1, :])
         word_pool = shared.tile([P, T], I32, name="word_pool", offset=0, align_bytes=64)
         nc.sync.dma_start(word_pool[:], k_words[0].rearrange("p t b -> p (t b)").bitcast(I32))
@@ -46,8 +46,6 @@ def tile_attend_link_age_topk_kernel(tc, qT, k_words, k_scales, ag, rt, offs, ou
         q_rows = qT[0].rearrange("(o p j) n -> o p j n", o=PASSES, j=PACK)
         for o in range(PASSES):
             nc.sync.dma_start(q_raw[o][:], q_rows[o])
-        rate = keep.tile([P, 1], F32, name="rate")
-        nc.sync.dma_start(rate[:], rt[0])
 
         one = keep.tile([P, 1], F32, name="one")
         nc.vector.memset(one[:], 1.0)
@@ -65,28 +63,33 @@ def tile_attend_link_age_topk_kernel(tc, qT, k_words, k_scales, ag, rt, offs, ou
 
         scale_rows = keep.tile([P, N], U8, name="scale_rows", align_bytes=64)
         nc.vector.tensor_copy(scale_rows[:], scale_pool[:].indirect(offsets[:]))
-
-        ages0 = keep.tile([P, N // 2], F32, name="ages0")
-        ages1 = shared.tile([P, N // 2], F32, name="ages1", offset=4 * T + 512, align_bytes=64)
-        ages = [ages0, ages1]
-        turned = [psum.tile([P, 2, P], F32, name=f"turned{h}") for h in range(2)]
-        spread = psum.tile([P, 4, P], F32, name="spread")
-        for h in range(2):
-            nc.scalar.activation(ages[h][:], age_pool[:].indirect(offsets[:, 16 * h : 16 * (h + 1)]), ACT.Copy)
-        k_planes = aged.tile([P, PASSES * N], U8, name="k_planes", offset=0, align_bytes=64)
+        k_planes = scaled.tile([P, PASSES * N], U8, name="k_planes", offset=0, align_bytes=64)
         for quad in range(4):
-            nc.scalar.dma_start(
+            nc.sync.dma_start(
                 k_planes[32 * quad : 32 * quad + 4, :].bitcast(I32),
                 scale_rows[96 + 8 * quad : 96 + 8 * (quad + 1), :].bitcast(I32),
             )
-        for h in range(2):
+        rate = scaled.tile([P, 1], F32, name="rate", offset=PASSES * N, align_bytes=64)
+        nc.sync.dma_start(rate[:], rt[0])
+
+        ages0 = keep.tile([P, N // 2], F32, name="ages0", align_bytes=64)
+        ages1 = shared.tile([P, N // 2], F32, name="ages1", offset=4 * T + 512, align_bytes=64)
+        ages = [ages0, ages1]
+        spread = psum.tile([P, 4, P], F32, name="spread")
+        nc.scalar.activation(ages[0][:], age_pool[:].indirect(offsets[:, 0:16]), ACT.Copy)
+        nc.vector.tensor_copy(ages[1][:], age_pool[:].indirect(offsets[:, 16:32]))
+
+        def spread_ages(h):
+            turned = psum.tile([P, 2, P], F32, name="turned")
             for c in range(2):
-                nc.tensor.transpose(turned[h][:, c, :], ages[h][:, c * P : (c + 1) * P], ident[:])
-        for h in range(2):
+                nc.tensor.transpose(turned[:, c, :], ages[h][:, c * P : (c + 1) * P], ident[:])
             age_cols = keep.tile([P, 2], F32, name=f"age_cols{h}")
-            nc.scalar.activation(age_cols[:], turned[h][:, :, AGE_ROW], ACT.Copy, scale=-1.0)
+            nc.scalar.activation(age_cols[:], turned[:, :, AGE_ROW], ACT.Copy, scale=-1.0)
             for c in range(2):
                 nc.tensor.transpose(spread[:, 2 * h + c, :], age_cols[:, c : c + 1].to_broadcast([P, P]), ident[:])
+
+        spread_ages(0)
+        spread_ages(1)
 
         q_bf = [
             shared.tile([P, NQ, PACK], BF16, name=f"q_bf{o}", offset=4 * T + 1024 * o, align_bytes=64)

@@ -34,15 +34,15 @@ def tile_attend_link_age_topk_kernel(tc, qT, k_words, k_scales, ag, rt, offs, ou
         scaled = ctx.enter_context(tc.tile_pool(name="scaled", bufs=1))
         psum = ctx.enter_context(tc.psum_pool(name="psum", bufs=1))
 
-        scale_pool = scaled.tile([P, T], U8, name="scale_pool", offset=0, align_bytes=64)
+        scale_pool = scaled.tile([P, T], U8, name="scale_pool", offset=0, align_bytes=512)
         nc.sync.dma_start(scale_pool[96:P, :].bitcast(I32), k_scales.bitcast(I32).rearrange("o f t -> f o t"))
         offsets = keep.tile([P, N // 16], U16, name="offsets")
         nc.sync.dma_start(offsets[:], offs)
-        age_pool = keep.tile([P, T], F32, name="age_pool", align_bytes=64)
+        age_pool = keep.tile([P, T], F32, name="age_pool", align_bytes=512)
         nc.sync.dma_start(age_pool[AGE_ROW:P, :], ag[0:1, :])
-        word_pool = shared.tile([P, T], I32, name="word_pool", offset=0, align_bytes=64)
+        word_pool = shared.tile([P, T], I32, name="word_pool", offset=0, align_bytes=512)
         nc.sync.dma_start(word_pool[:], k_words[0].rearrange("p t b -> p (t b)").bitcast(I32))
-        q_raw = [keep.tile([P, PACK, NQ], F32, name=f"q_raw{o}") for o in range(PASSES)]
+        q_raw = [keep.tile([P, PACK, NQ], F32, name=f"q_raw{o}", align_bytes=512) for o in range(PASSES)]
         q_rows = qT[0].rearrange("(o p j) n -> o p j n", o=PASSES, j=PACK)
         for o in range(PASSES):
             nc.sync.dma_start(q_raw[o][:], q_rows[o])
@@ -61,7 +61,7 @@ def tile_attend_link_age_topk_kernel(tc, qT, k_words, k_scales, ag, rt, offs, ou
         ident = keep.tile([P, P], F32, name="ident")
         make_identity(nc, ident[:])
 
-        scale_rows = keep.tile([P, N], U8, name="scale_rows", align_bytes=64)
+        scale_rows = keep.tile([P, N], U8, name="scale_rows", align_bytes=512)
         nc.vector.tensor_copy(scale_rows[:], scale_pool[:].indirect(offsets[:]))
         k_planes = scaled.tile([P, PASSES * N], U8, name="k_planes", offset=0, align_bytes=64)
         for quad in range(4):
@@ -102,7 +102,7 @@ def tile_attend_link_age_topk_kernel(tc, qT, k_words, k_scales, ag, rt, offs, ou
                 ACT.Copy,
             )
 
-        words = [keep.tile([P, N // 2], U32, name=f"words{h}", align_bytes=64) for h in range(2)]
+        words = [keep.tile([P, N // 2], U32, name=f"words{h}", align_bytes=256) for h in range(2)]
         for h in range(2):
             nc.vector.tensor_copy(words[h][:], word_pool[:].bitcast(U32).indirect(offsets[:, 16 * h : 16 * (h + 1)]))
 
@@ -116,7 +116,7 @@ def tile_attend_link_age_topk_kernel(tc, qT, k_words, k_scales, ag, rt, offs, ou
             )
 
         def part(o, first, count):
-            codes = keep.tile([P, count * 2 * P], U8, name=f"codes{o}{first}", align_bytes=64)
+            codes = keep.tile([P, count * 2 * P], U8, name=f"codes{o}{first}", align_bytes=256)
             src = words[first // 2][:, P * (first % 2) : P * (first % 2 + count)]
             nc.vector.tensor_copy(codes[:].bitcast(U16), src.bitcast(U16).rearrange("p (n o) -> p o n", o=PASSES)[:, o, :])
             for i in range(count):
@@ -148,7 +148,7 @@ def tile_attend_link_age_topk_kernel(tc, qT, k_words, k_scales, ag, rt, offs, ou
                     stop=(o == PASSES - 1),
                 )
 
-        res = [keep.tile([P, 2, P], F32, name=f"res{h}") for h in range(2)]
+        res = [keep.tile([P, 2, P], F32, name=f"res{h}", align_bytes=512) for h in range(2)]
         pieces = [(0, P), (P, 2 * P), (2 * P, 3 * P), (3 * P, 3 * P + P // 2), (3 * P + P // 2, N)]
         for lo, hi in pieces:
             c = lo // P

@@ -32,6 +32,7 @@ def tile_attend_link_age_topk_kernel(tc, qT, k_words, k_scales, ag, rt, offs, ou
         keep = ctx.enter_context(tc.tile_pool(name="keep", bufs=1))
         shared = ctx.enter_context(tc.tile_pool(name="shared", bufs=1))
         scaled = ctx.enter_context(tc.tile_pool(name="scaled", bufs=1))
+        late = ctx.enter_context(tc.tile_pool(name="late", bufs=1))
         psum = ctx.enter_context(tc.psum_pool(name="psum", bufs=1))
 
         scale_pool = scaled.tile([P, T], U8, name="scale_pool", offset=0, align_bytes=512)
@@ -42,7 +43,9 @@ def tile_attend_link_age_topk_kernel(tc, qT, k_words, k_scales, ag, rt, offs, ou
         nc.sync.dma_start(age_pool[AGE_ROW:P, :], ag[0:1, :])
         word_pool = shared.tile([P, T], I32, name="word_pool", offset=0, align_bytes=512)
         nc.sync.dma_start(word_pool[:], k_words[0].rearrange("p t b -> p (t b)").bitcast(I32))
-        q_raw = [keep.tile([P, PACK, NQ], F32, name=f"q_raw{o}", align_bytes=512) for o in range(PASSES)]
+        q_raw = [
+            late.tile([P, PACK, NQ], F32, name=f"q_raw{o}", offset=2048 * o, align_bytes=512) for o in range(PASSES)
+        ]
         q_rows = qT[0].rearrange("(o p j) n -> o p j n", o=PASSES, j=PACK)
         for o in range(PASSES):
             nc.sync.dma_start(q_raw[o][:], q_rows[o])
@@ -115,20 +118,20 @@ def tile_attend_link_age_topk_kernel(tc, qT, k_words, k_scales, ag, rt, offs, ou
                 out=q_codes[o][:].bitcast(FP8X4), scales=q_planes[o][:], in_=q_bf[o][:].rearrange("p n j -> p (n j)")
             )
 
-        def part(o, first, count):
-            codes = keep.tile([P, count * 2 * P], U8, name=f"codes{o}{first}", align_bytes=256)
+        def part(o, first, count, place):
+            codes = late.tile([P, count * 2 * P], U8, name=f"codes{o}{first}", offset=place, align_bytes=256)
             src = words[first // 2][:, P * (first % 2) : P * (first % 2 + count)]
             nc.vector.tensor_copy(codes[:].bitcast(U16), src.bitcast(U16).rearrange("p (n o) -> p o n", o=PASSES)[:, o, :])
             for i in range(count):
                 k_codes[(first + i, o)] = codes[:, 2 * P * i : 2 * P * (i + 1)]
 
-        part(0, 0, 2)
+        part(0, 0, 2, 4096)
         quantize(0)
-        part(0, 2, 2)
-        part(1, 0, 2)
+        part(0, 2, 2, 0)
+        part(1, 0, 2, 512)
         quantize(1)
-        part(1, 2, 1)
-        part(1, 3, 1)
+        part(1, 2, 1, 2048)
+        part(1, 3, 1, 2304)
 
         half_decay = keep.tile([P, N], F32, name="half_decay")
         nc.scalar.activation(

@@ -40,7 +40,7 @@ def tile_attend_link_age_topk_kernel(tc, qT, k_words, k_scales, ag, rt, offs, ou
         offsets = keep.tile([P, N // 16], U16, name="offsets")
         nc.sync.dma_start(offsets[:], offs)
         age_pool = keep.tile([P, T], F32, name="age_pool", align_bytes=512)
-        nc.sync.dma_start(age_pool[AGE_ROW:P, :], ag[0:1, :])
+        nc.scalar.dma_start(age_pool[AGE_ROW:P, :], ag[0:1, :])
         word_pool = shared.tile([P, T], I32, name="word_pool", offset=0, align_bytes=512)
         nc.sync.dma_start(word_pool[:], k_words[0].rearrange("p t b -> p (t b)").bitcast(I32))
         q_raw = [
@@ -75,24 +75,20 @@ def tile_attend_link_age_topk_kernel(tc, qT, k_words, k_scales, ag, rt, offs, ou
         rate = scaled.tile([P, 1], F32, name="rate", offset=PASSES * N, align_bytes=64)
         nc.sync.dma_start(rate[:], rt[0])
 
-        ages0 = keep.tile([P, N // 2], F32, name="ages0", align_bytes=64)
-        ages1 = shared.tile([P, N // 2], F32, name="ages1", offset=4 * T + 512, align_bytes=64)
-        ages = [ages0, ages1]
+        ages0 = keep.tile([P, 2 * P], F32, name="ages0", align_bytes=64)
+        ages1 = keep.tile([P, P], F32, name="ages1", align_bytes=64)
+        ages2 = shared.tile([P, P], F32, name="ages2", offset=4 * T + 768, align_bytes=64)
+        nc.scalar.activation(ages0[:], age_pool[:].indirect(offsets[:, 0:16]), ACT.Copy)
+        nc.scalar.activation(ages1[:], age_pool[:].indirect(offsets[:, 16:24]), ACT.Copy)
+        nc.vector.tensor_copy(ages2[:], age_pool[:].indirect(offsets[:, 24:32]))
+        turned = psum.tile([P, 4, P], F32, name="turned")
+        for c, block in enumerate((ages0[:, 0:P], ages0[:, P : 2 * P], ages1[:], ages2[:])):
+            nc.tensor.transpose(turned[:, c, :], block, ident[:])
+        age_cols = keep.tile([P, 4], F32, name="age_cols")
+        nc.scalar.activation(age_cols[:], turned[:, :, AGE_ROW], ACT.Copy, scale=-1.0)
         spread = psum.tile([P, 4, P], F32, name="spread")
-        nc.scalar.activation(ages[0][:], age_pool[:].indirect(offsets[:, 0:16]), ACT.Copy)
-        nc.vector.tensor_copy(ages[1][:], age_pool[:].indirect(offsets[:, 16:32]))
-
-        def spread_ages(h):
-            turned = psum.tile([P, 2, P], F32, name="turned")
-            for c in range(2):
-                nc.tensor.transpose(turned[:, c, :], ages[h][:, c * P : (c + 1) * P], ident[:])
-            age_cols = keep.tile([P, 2], F32, name=f"age_cols{h}")
-            nc.scalar.activation(age_cols[:], turned[:, :, AGE_ROW], ACT.Copy, scale=-1.0)
-            for c in range(2):
-                nc.tensor.transpose(spread[:, 2 * h + c, :], age_cols[:, c : c + 1].to_broadcast([P, P]), ident[:])
-
-        spread_ages(0)
-        spread_ages(1)
+        for c in range(4):
+            nc.tensor.transpose(spread[:, c, :], age_cols[:, c : c + 1].to_broadcast([P, P]), ident[:])
 
         q_bf = [
             shared.tile([P, NQ, PACK], BF16, name=f"q_bf{o}", offset=4 * T + 1024 * o, align_bytes=64)

@@ -33,6 +33,7 @@ def tile_attend_link_age_topk_kernel(tc, qT, k_words, k_scales, ag, rt, offs, ou
         shared = ctx.enter_context(tc.tile_pool(name="shared", bufs=1))
         scaled = ctx.enter_context(tc.tile_pool(name="scaled", bufs=1))
         late = ctx.enter_context(tc.tile_pool(name="late", bufs=1))
+        aged = ctx.enter_context(tc.tile_pool(name="aged", bufs=1))
         psum = ctx.enter_context(tc.psum_pool(name="psum", bufs=1))
 
         scale_pool = scaled.tile([P, T], U8, name="scale_pool", offset=0, align_bytes=512)
@@ -75,23 +76,21 @@ def tile_attend_link_age_topk_kernel(tc, qT, k_words, k_scales, ag, rt, offs, ou
         rate = scaled.tile([P, 1], F32, name="rate", offset=PASSES * N, align_bytes=64)
         nc.sync.dma_start(rate[:], rt[0])
 
-        ages0 = keep.tile([P, 2 * P], F32, name="ages0", align_bytes=64)
-        ages1 = keep.tile([P, P], F32, name="ages1", align_bytes=64)
-        ages2 = shared.tile([P, P], F32, name="ages2", offset=4 * T + 768, align_bytes=64)
-        nc.scalar.activation(ages0[:], age_pool[:].indirect(offsets[:, 0:16]), ACT.Copy)
-        nc.scalar.activation(ages1[:], age_pool[:].indirect(offsets[:, 16:24]), ACT.Copy)
-        nc.vector.tensor_copy(ages2[:], age_pool[:].indirect(offsets[:, 24:32]))
+        ages = aged.tile([P, N], F32, name="ages", offset=768, align_bytes=256)
+        nc.scalar.activation(ages[:, 0 : 2 * P], age_pool[:].indirect(offsets[:, 0:16]), ACT.Copy)
+        nc.scalar.activation(ages[:, 2 * P : 3 * P], age_pool[:].indirect(offsets[:, 16:24]), ACT.Copy)
+        nc.vector.tensor_copy(ages[:, 3 * P : N], age_pool[:].indirect(offsets[:, 24:32]))
         turned = psum.tile([P, 4, P], F32, name="turned")
-        for c, block in enumerate((ages0[:, 0:P], ages0[:, P : 2 * P], ages1[:], ages2[:])):
-            nc.tensor.transpose(turned[:, c, :], block, ident[:])
+        for c in range(4):
+            nc.tensor.transpose(turned[:, c, :], ages[:, c * P : (c + 1) * P], ident[:])
         age_cols = keep.tile([P, 4], F32, name="age_cols")
-        nc.scalar.activation(age_cols[:], turned[:, :, AGE_ROW], ACT.Copy, scale=-1.0)
+        nc.vector.tensor_scalar(age_cols[:], turned[:, :, AGE_ROW], -1.0, None, ALU.mult)
         spread = psum.tile([P, 4, P], F32, name="spread")
         for c in range(4):
             nc.tensor.transpose(spread[:, c, :], age_cols[:, c : c + 1].to_broadcast([P, P]), ident[:])
 
         q_bf = [
-            shared.tile([P, NQ, PACK], BF16, name=f"q_bf{o}", offset=4 * T + 1024 * o, align_bytes=64)
+            aged.tile([P, NQ, PACK], BF16, name=f"q_bf{o}", offset=2560 * o, align_bytes=256)
             for o in range(PASSES)
         ]
         for o in range(PASSES):
@@ -101,7 +100,9 @@ def tile_attend_link_age_topk_kernel(tc, qT, k_words, k_scales, ag, rt, offs, ou
                 ACT.Copy,
             )
 
-        words = [keep.tile([P, N // 2], U32, name=f"words{h}", align_bytes=256) for h in range(2)]
+        words0 = keep.tile([P, N // 2], U32, name="words0", align_bytes=256)
+        words1 = aged.tile([P, N // 2], U32, name="words1", offset=1024, align_bytes=256)
+        words = [words0, words1]
         for h in range(2):
             nc.vector.tensor_copy(words[h][:], word_pool[:].bitcast(U32).indirect(offsets[:, 16 * h : 16 * (h + 1)]))
 
@@ -114,20 +115,20 @@ def tile_attend_link_age_topk_kernel(tc, qT, k_words, k_scales, ag, rt, offs, ou
                 out=q_codes[o][:].bitcast(FP8X4), scales=q_planes[o][:], in_=q_bf[o][:].rearrange("p n j -> p (n j)")
             )
 
-        def part(o, first, count, place):
-            codes = late.tile([P, count * 2 * P], U8, name=f"codes{o}{first}", offset=place, align_bytes=256)
+        def part(o, first, count, pool, place):
+            codes = pool.tile([P, count * 2 * P], U8, name=f"codes{o}{first}", offset=place, align_bytes=256)
             src = words[first // 2][:, P * (first % 2) : P * (first % 2 + count)]
             nc.vector.tensor_copy(codes[:].bitcast(U16), src.bitcast(U16).rearrange("p (n o) -> p o n", o=PASSES)[:, o, :])
             for i in range(count):
                 k_codes[(first + i, o)] = codes[:, 2 * P * i : 2 * P * (i + 1)]
 
-        part(0, 0, 2, 4096)
+        part(0, 0, 2, aged, 2048)
         quantize(0)
-        part(0, 2, 2, 0)
-        part(1, 0, 2, 512)
+        part(0, 2, 2, late, 0)
+        part(1, 0, 2, late, 512)
         quantize(1)
-        part(1, 2, 1, 2048)
-        part(1, 3, 1, 2304)
+        part(1, 2, 1, late, 2048)
+        part(1, 3, 1, late, 2304)
 
         half_decay = keep.tile([P, N], F32, name="half_decay")
         nc.scalar.activation(

@@ -22,7 +22,7 @@ NQ = 128
 PASSES = 2
 PACK = 4
 AGE_ROW = 127
-AGE_SPLIT = 768
+AGE_SPLIT = 512
 FLOPS = 2 * 1024 * NQ * N
 
 
@@ -34,13 +34,14 @@ def tile_attend_link_age_topk_kernel(tc, qT, k_words, k_scales, ag, rt, offs, ou
         scaled = ctx.enter_context(tc.tile_pool(name="scaled", bufs=1))
         late = ctx.enter_context(tc.tile_pool(name="late", bufs=1))
         aged = ctx.enter_context(tc.tile_pool(name="aged", bufs=1))
+        cast = ctx.enter_context(tc.tile_pool(name="cast", bufs=1))
         psum = ctx.enter_context(tc.psum_pool(name="psum", bufs=1))
 
         scale_pool = scaled.tile([P, T], U8, name="scale_pool", offset=0, align_bytes=512)
-        nc.sync.dma_start(scale_pool[96:P, :].bitcast(I32), k_scales.bitcast(I32).rearrange("o f t -> f o t"))
+        nc.sync.dma_start(scale_pool[32:64, :].bitcast(I32), k_scales.bitcast(I32).rearrange("o f t -> f o t"))
         offsets = keep.tile([P, N // 16], U16, name="offsets")
         nc.sync.dma_start(offsets[:], offs)
-        age_pool = keep.tile([P, T], F32, name="age_pool", align_bytes=512)
+        age_pool = cast.tile([P, T], F32, name="age_pool", offset=0, align_bytes=512)
         nc.scalar.dma_start(age_pool[AGE_ROW:P, :], ag[0:1, :])
         word_pool = shared.tile([P, T], I32, name="word_pool", offset=0, align_bytes=512)
         nc.sync.dma_start(word_pool[:], k_words[0].rearrange("p t b -> p (t b)").bitcast(I32))
@@ -56,9 +57,10 @@ def tile_attend_link_age_topk_kernel(tc, qT, k_words, k_scales, ag, rt, offs, ou
         log_half = keep.tile([P, 1], F32, name="log_half")
         nc.scalar.activation(log_half[:], one[:], ACT.Copy, scale=-math.log(2.0))
 
-        scale_words = scale_pool[0:96, :].bitcast(I32)
+        scale_above = scale_pool[0:32, :].bitcast(I32)
+        scale_below = scale_pool[64:P, :].bitcast(I32)
         age_words = age_pool[0:AGE_ROW, :].bitcast(I32)
-        for region, lo, mid, hi in ((scale_words, 0, 255, 512), (age_words, 0, 511, AGE_SPLIT)):
+        for region, lo, mid, hi in ((scale_above, 0, 255, 512), (scale_below, 0, 255, 512), (age_words, 0, 255, AGE_SPLIT)):
             nc.vector.memset(region[:, lo:mid], 0)
             nc.vector.memset(region[:, mid:hi], 0)
         nc.gpsimd.memset(age_words[:, AGE_SPLIT:T], 0)
@@ -71,12 +73,12 @@ def tile_attend_link_age_topk_kernel(tc, qT, k_words, k_scales, ag, rt, offs, ou
         for quad in range(4):
             nc.sync.dma_start(
                 k_planes[32 * quad : 32 * quad + 4, :].bitcast(I32),
-                scale_rows[96 + 8 * quad : 96 + 8 * (quad + 1), :].bitcast(I32),
+                scale_rows[32 + 8 * quad : 32 + 8 * (quad + 1), :].bitcast(I32),
             )
         rate = scaled.tile([P, 1], F32, name="rate", offset=PASSES * N, align_bytes=64)
         nc.sync.dma_start(rate[:], rt[0])
 
-        ages = aged.tile([P, N], F32, name="ages", offset=768, align_bytes=256)
+        ages = aged.tile([P, N], F32, name="ages", offset=0, align_bytes=256)
         nc.scalar.activation(ages[:, 0 : 2 * P], age_pool[:].indirect(offsets[:, 0:16]), ACT.Copy)
         nc.scalar.activation(ages[:, 2 * P : 3 * P], age_pool[:].indirect(offsets[:, 16:24]), ACT.Copy)
         nc.vector.tensor_copy(ages[:, 3 * P : N], age_pool[:].indirect(offsets[:, 24:32]))
@@ -90,7 +92,7 @@ def tile_attend_link_age_topk_kernel(tc, qT, k_words, k_scales, ag, rt, offs, ou
             nc.tensor.transpose(spread[:, c, :], age_cols[:, c : c + 1].to_broadcast([P, P]), ident[:])
 
         q_bf = [
-            aged.tile([P, NQ, PACK], BF16, name=f"q_bf{o}", offset=2560 * o, align_bytes=256)
+            cast.tile([P, NQ, PACK], BF16, name=f"q_bf{o}", offset=1024 * o, align_bytes=256)
             for o in range(PASSES)
         ]
         for o in range(PASSES):
@@ -101,7 +103,7 @@ def tile_attend_link_age_topk_kernel(tc, qT, k_words, k_scales, ag, rt, offs, ou
             )
 
         words0 = keep.tile([P, N // 2], U32, name="words0", align_bytes=256)
-        words1 = aged.tile([P, N // 2], U32, name="words1", offset=1024, align_bytes=256)
+        words1 = aged.tile([P, N // 2], U32, name="words1", offset=0, align_bytes=256)
         words = [words0, words1]
         for h in range(2):
             nc.vector.tensor_copy(words[h][:], word_pool[:].bitcast(U32).indirect(offsets[:, 16 * h : 16 * (h + 1)]))
@@ -122,10 +124,10 @@ def tile_attend_link_age_topk_kernel(tc, qT, k_words, k_scales, ag, rt, offs, ou
             for i in range(count):
                 k_codes[(first + i, o)] = codes[:, 2 * P * i : 2 * P * (i + 1)]
 
-        part(0, 0, 2, aged, 2048)
+        part(0, 0, 2, aged, 1024)
         quantize(0)
         part(0, 2, 2, late, 0)
-        part(1, 0, 2, late, 512)
+        part(1, 0, 2, aged, 1536)
         quantize(1)
         part(1, 2, 1, late, 2048)
         part(1, 3, 1, late, 2304)

@@ -22,7 +22,7 @@ NQ = 128
 PASSES = 2
 PACK = 4
 AGE_ROW = 127
-AGE_SPLIT = 512
+AGE_SPLIT = 384
 FLOPS = 2 * 1024 * NQ * N
 
 
@@ -60,7 +60,7 @@ def tile_attend_link_age_topk_kernel(tc, qT, k_words, k_scales, ag, rt, offs, ou
         scale_above = scale_pool[0:32, :].bitcast(I32)
         scale_below = scale_pool[64:P, :].bitcast(I32)
         age_words = age_pool[0:AGE_ROW, :].bitcast(I32)
-        for region, lo, mid, hi in ((scale_above, 0, 255, 512), (scale_below, 0, 255, 512), (age_words, 0, 255, AGE_SPLIT)):
+        for region, lo, mid, hi in ((scale_above, 0, 255, 512), (scale_below, 0, 255, 512), (age_words, 0, 127, AGE_SPLIT)):
             nc.vector.memset(region[:, lo:mid], 0)
             nc.vector.memset(region[:, mid:hi], 0)
         nc.gpsimd.memset(age_words[:, AGE_SPLIT:T], 0)
@@ -80,8 +80,8 @@ def tile_attend_link_age_topk_kernel(tc, qT, k_words, k_scales, ag, rt, offs, ou
 
         ages = aged.tile([P, N], F32, name="ages", offset=0, align_bytes=256)
         nc.scalar.activation(ages[:, 0 : 2 * P], age_pool[:].indirect(offsets[:, 0:16]), ACT.Copy)
-        nc.scalar.activation(ages[:, 2 * P : 3 * P], age_pool[:].indirect(offsets[:, 16:24]), ACT.Copy)
-        nc.vector.tensor_copy(ages[:, 3 * P : N], age_pool[:].indirect(offsets[:, 24:32]))
+        nc.vector.tensor_copy(ages[:, 2 * P : 3 * P], age_pool[:].indirect(offsets[:, 16:24]))
+        nc.scalar.activation(ages[:, 3 * P : N], age_pool[:].indirect(offsets[:, 24:32]), ACT.Copy)
         turned = psum.tile([P, 4, P], F32, name="turned")
         for c in range(4):
             nc.tensor.transpose(turned[:, c, :], ages[:, c * P : (c + 1) * P], ident[:])

@@ -23,6 +23,7 @@ PASSES = 2
 PACK = 4
 AGE_ROW = 127
 AGE_SPLIT = 384
+SCALAR_COLS = 96
 FLOPS = 2 * 1024 * NQ * N
 
 
@@ -34,14 +35,13 @@ def tile_attend_link_age_topk_kernel(tc, qT, k_words, k_scales, ag, rt, offs, ou
         scaled = ctx.enter_context(tc.tile_pool(name="scaled", bufs=1))
         late = ctx.enter_context(tc.tile_pool(name="late", bufs=1))
         aged = ctx.enter_context(tc.tile_pool(name="aged", bufs=1))
-        cast = ctx.enter_context(tc.tile_pool(name="cast", bufs=1))
         psum = ctx.enter_context(tc.psum_pool(name="psum", bufs=1))
 
         scale_pool = scaled.tile([P, T], U8, name="scale_pool", offset=0, align_bytes=512)
         nc.sync.dma_start(scale_pool[32:64, :].bitcast(I32), k_scales.bitcast(I32).rearrange("o f t -> f o t"))
         offsets = keep.tile([P, N // 16], U16, name="offsets")
         nc.sync.dma_start(offsets[:], offs)
-        age_pool = cast.tile([P, T], F32, name="age_pool", offset=0, align_bytes=512)
+        age_pool = keep.tile([P, T], F32, name="age_pool", align_bytes=512)
         nc.scalar.dma_start(age_pool[AGE_ROW:P, :], ag[0:1, :])
         word_pool = shared.tile([P, T], I32, name="word_pool", offset=0, align_bytes=512)
         nc.sync.dma_start(word_pool[:], k_words[0].rearrange("p t b -> p (t b)").bitcast(I32))
@@ -86,25 +86,23 @@ def tile_attend_link_age_topk_kernel(tc, qT, k_words, k_scales, ag, rt, offs, ou
         for c in range(4):
             nc.tensor.transpose(turned[:, c, :], ages[:, c * P : (c + 1) * P], ident[:])
         age_cols = keep.tile([P, 4], F32, name="age_cols")
-        nc.vector.tensor_scalar(age_cols[:], turned[:, :, AGE_ROW], -1.0, None, ALU.mult)
+        nc.scalar.activation(age_cols[:], turned[:, :, AGE_ROW], ACT.Copy, scale=-1.0)
         spread = psum.tile([P, 4, P], F32, name="spread")
         for c in range(4):
             nc.tensor.transpose(spread[:, c, :], age_cols[:, c : c + 1].to_broadcast([P, P]), ident[:])
 
         q_bf = [
-            cast.tile([P, NQ, PACK], BF16, name=f"q_bf{o}", offset=1024 * o, align_bytes=256)
-            for o in range(PASSES)
+            aged.tile([P, NQ * PACK], BF16, name=f"q_bf{o}", offset=1024 * o, align_bytes=256) for o in range(PASSES)
         ]
-        for o in range(PASSES):
-            nc.scalar.activation(
-                q_bf[o][:].rearrange("p (c i) j -> p c j i", i=4),
-                q_raw[o][:].rearrange("p j (c i) -> p c j i", i=4),
-                ACT.Copy,
-            )
 
-        words0 = keep.tile([P, N // 2], U32, name="words0", align_bytes=256)
-        words1 = aged.tile([P, N // 2], U32, name="words1", offset=0, align_bytes=256)
-        words = [words0, words1]
+        def lines(o, lo, hi):
+            dst = q_bf[o][:, PACK * lo : PACK * hi].rearrange("p (c i j) -> p c j i", i=4, j=PACK)
+            return dst, q_raw[o][:, :, lo:hi].rearrange("p j (c i) -> p c j i", i=4)
+
+        nc.scalar.activation(*lines(0, 0, NQ), ACT.Copy)
+        nc.scalar.activation(*lines(1, 0, SCALAR_COLS), ACT.Copy)
+
+        words = [keep.tile([P, N // 2], U32, name=f"words{h}", align_bytes=256) for h in range(2)]
         for h in range(2):
             nc.vector.tensor_copy(words[h][:], word_pool[:].bitcast(U32).indirect(offsets[:, 16 * h : 16 * (h + 1)]))
 
@@ -114,7 +112,7 @@ def tile_attend_link_age_topk_kernel(tc, qT, k_words, k_scales, ag, rt, offs, ou
 
         def quantize(o):
             nc.vector.quantize_mx(
-                out=q_codes[o][:].bitcast(FP8X4), scales=q_planes[o][:], in_=q_bf[o][:].rearrange("p n j -> p (n j)")
+                out=q_codes[o][:].bitcast(FP8X4), scales=q_planes[o][:], in_=q_bf[o][:]
             )
 
         def part(o, first, count, pool, place):
@@ -124,13 +122,20 @@ def tile_attend_link_age_topk_kernel(tc, qT, k_words, k_scales, ag, rt, offs, ou
             for i in range(count):
                 k_codes[(first + i, o)] = codes[:, 2 * P * i : 2 * P * (i + 1)]
 
-        part(0, 0, 2, aged, 1024)
+        part(0, 0, 2, late, 4096)
+        nc.vector.tensor_copy(*lines(1, SCALAR_COLS, NQ))
         quantize(0)
-        part(0, 2, 2, late, 0)
-        part(1, 0, 2, aged, 1536)
+        part(0, 2, 1, late, 0)
+        part(1, 0, 1, late, 256)
         quantize(1)
-        part(1, 2, 1, late, 2048)
-        part(1, 3, 1, late, 2304)
+        part(1, 1, 1, late, 2048)
+        part(1, 2, 1, late, 2304)
+        last = late.tile([P, PASSES, 2 * P], U8, name="codes3", offset=2560, align_bytes=256)
+        nc.vector.tensor_copy(
+            last[:].bitcast(U16), words[1][:, P : 2 * P].bitcast(U16).rearrange("p (n o) -> p o n", o=PASSES)
+        )
+        for o in range(PASSES):
+            k_codes[(3, o)] = last[:, o, :]
 
         half_decay = keep.tile([P, N], F32, name="half_decay")
         nc.scalar.activation(
@@ -138,17 +143,16 @@ def tile_attend_link_age_topk_kernel(tc, qT, k_words, k_scales, ag, rt, offs, ou
         )
 
         scores = [psum.tile([P, P], F32, name=f"scores{c}") for c in range(4)]
-        for o in range(PASSES):
-            for c in range(4):
-                nc.tensor.matmul_mx(
-                    out=scores[c][:],
-                    lhsT=q_codes[o][:].bitcast(FP8X4),
-                    lhsT_scale=q_planes[o][:],
-                    rhs=k_codes[(c, o)].bitcast(FP4X4),
-                    rhs_scale=k_planes[:, o * N + P * c : o * N + P * (c + 1)],
-                    start=(o == 0),
-                    stop=(o == PASSES - 1),
-                )
+        for c, o in [(c, o) for o in range(PASSES) for c in range(3)] + [(3, o) for o in range(PASSES)]:
+            nc.tensor.matmul_mx(
+                out=scores[c][:],
+                lhsT=q_codes[o][:].bitcast(FP8X4),
+                lhsT_scale=q_planes[o][:],
+                rhs=k_codes[(c, o)].bitcast(FP4X4),
+                rhs_scale=k_planes[:, o * N + P * c : o * N + P * (c + 1)],
+                start=(o == 0),
+                stop=(o == PASSES - 1),
+            )
 
         res = [keep.tile([P, 2, P], F32, name=f"res{h}", align_bytes=512) for h in range(2)]
         pieces = [(0, P), (P, 2 * P), (2 * P, 3 * P), (3 * P, 3 * P + P // 2), (3 * P + P // 2, N)]

@@ -51,6 +51,8 @@ def tile_attend_link_age_topk_kernel(tc, qT, k_words, k_scales, ag, rt, offs, ou
         q_rows = qT[0].rearrange("(o p j) n -> o p j n", o=PASSES, j=PACK)
         for o in range(PASSES):
             nc.sync.dma_start(q_raw[o][:], q_rows[o])
+        rate = keep.tile([P, 1], F32, name="rate", align_bytes=64)
+        nc.sync.dma_start(rate[:], rt[0])
 
         one = keep.tile([P, 1], F32, name="one")
         nc.vector.memset(one[:], 1.0)
@@ -75,8 +77,6 @@ def tile_attend_link_age_topk_kernel(tc, qT, k_words, k_scales, ag, rt, offs, ou
                 k_planes[32 * quad : 32 * quad + 4, :].bitcast(I32),
                 scale_rows[32 + 8 * quad : 32 + 8 * (quad + 1), :].bitcast(I32),
             )
-        rate = scaled.tile([P, 1], F32, name="rate", offset=PASSES * N, align_bytes=64)
-        nc.sync.dma_start(rate[:], rt[0])
 
         ages = aged.tile([P, N], F32, name="ages", offset=0, align_bytes=256)
         nc.scalar.activation(ages[:, 0 : 2 * P], age_pool[:].indirect(offsets[:, 0:16]), ACT.Copy)

@@ -82,14 +82,18 @@ def tile_attend_link_age_topk_kernel(tc, qT, k_words, k_scales, ag, rt, offs, ou
         nc.scalar.activation(ages[:, 0 : 2 * P], age_pool[:].indirect(offsets[:, 0:16]), ACT.Copy)
         nc.vector.tensor_copy(ages[:, 2 * P : 3 * P], age_pool[:].indirect(offsets[:, 16:24]))
         nc.scalar.activation(ages[:, 3 * P : N], age_pool[:].indirect(offsets[:, 24:32]), ACT.Copy)
-        turned = psum.tile([P, 4, P], F32, name="turned")
-        for c in range(4):
-            nc.tensor.transpose(turned[:, c, :], ages[:, c * P : (c + 1) * P], ident[:])
-        age_cols = keep.tile([P, 4], F32, name="age_cols")
-        nc.scalar.activation(age_cols[:], turned[:, :, AGE_ROW], ACT.Copy, scale=-1.0)
         spread = psum.tile([P, 4, P], F32, name="spread")
+        age_cols = []
+        for h in range(2):
+            turned = psum.tile([P, 2, P], F32, name=f"turned{h}")
+            for i in range(2):
+                c = 2 * h + i
+                nc.tensor.transpose(turned[:, i, :], ages[:, c * P : (c + 1) * P], ident[:])
+            cols = keep.tile([P, 2], F32, name=f"age_cols{h}")
+            nc.scalar.activation(cols[:], turned[:, :, AGE_ROW], ACT.Copy, scale=-1.0)
+            age_cols.append(cols)
         for c in range(4):
-            nc.tensor.transpose(spread[:, c, :], age_cols[:, c : c + 1].to_broadcast([P, P]), ident[:])
+            nc.tensor.transpose(spread[:, c, :], age_cols[c // 2][:, c % 2 : c % 2 + 1].to_broadcast([P, P]), ident[:])
 
         q_bf = [
             aged.tile([P, NQ * PACK], BF16, name=f"q_bf{o}", offset=1024 * o, align_bytes=256) for o in range(PASSES)

@@ -23,7 +23,8 @@ PASSES = 2
 PACK = 4
 AGE_ROW = 127
 AGE_SPLIT = 384
-SCALAR_COLS = 96
+SCALAR_COLS = 80
+EARLY_COLS = 48
 FLOPS = 2 * 1024 * NQ * N
 
 
@@ -78,22 +79,14 @@ def tile_attend_link_age_topk_kernel(tc, qT, k_words, k_scales, ag, rt, offs, ou
                 scale_rows[32 + 8 * quad : 32 + 8 * (quad + 1), :].bitcast(I32),
             )
 
-        ages = aged.tile([P, N], F32, name="ages", offset=0, align_bytes=256)
-        nc.scalar.activation(ages[:, 0 : 2 * P], age_pool[:].indirect(offsets[:, 0:16]), ACT.Copy)
-        nc.vector.tensor_copy(ages[:, 2 * P : 3 * P], age_pool[:].indirect(offsets[:, 16:24]))
-        nc.scalar.activation(ages[:, 3 * P : N], age_pool[:].indirect(offsets[:, 24:32]), ACT.Copy)
-        spread = psum.tile([P, 4, P], F32, name="spread")
-        age_cols = []
-        for h in range(2):
-            turned = psum.tile([P, 2, P], F32, name=f"turned{h}")
-            for i in range(2):
-                c = 2 * h + i
-                nc.tensor.transpose(turned[:, i, :], ages[:, c * P : (c + 1) * P], ident[:])
-            cols = keep.tile([P, 2], F32, name=f"age_cols{h}")
-            nc.scalar.activation(cols[:], turned[:, :, AGE_ROW], ACT.Copy, scale=-1.0)
-            age_cols.append(cols)
+        ages = [aged.tile([P, 2 * P], F32, name=f"ages{h}", offset=1024 * h, align_bytes=256) for h in range(2)]
+        nc.scalar.activation(ages[0][:], age_pool[:].indirect(offsets[:, 0:16]), ACT.Copy)
+        nc.vector.tensor_copy(ages[1][:, 0:P], age_pool[:].indirect(offsets[:, 16:24]))
+        nc.scalar.activation(ages[1][:, P : 2 * P], age_pool[:].indirect(offsets[:, 24:32]), ACT.Copy)
+        turned = [psum.tile([P, 2, P], F32, name=f"turned{h}") for h in range(2)]
         for c in range(4):
-            nc.tensor.transpose(spread[:, c, :], age_cols[c // 2][:, c % 2 : c % 2 + 1].to_broadcast([P, P]), ident[:])
+            nc.tensor.transpose(turned[c // 2][:, c % 2, :], ages[c // 2][:, (c % 2) * P : (c % 2 + 1) * P], ident[:])
+        age_cols = [keep.tile([P, 2], F32, name=f"age_cols{h}") for h in range(2)]
 
         q_bf = [
             aged.tile([P, NQ * PACK], BF16, name=f"q_bf{o}", offset=1024 * o, align_bytes=256) for o in range(PASSES)
@@ -103,8 +96,15 @@ def tile_attend_link_age_topk_kernel(tc, qT, k_words, k_scales, ag, rt, offs, ou
             dst = q_bf[o][:, PACK * lo : PACK * hi].rearrange("p (c i j) -> p c j i", i=4, j=PACK)
             return dst, q_raw[o][:, :, lo:hi].rearrange("p j (c i) -> p c j i", i=4)
 
-        nc.scalar.activation(*lines(0, 0, NQ), ACT.Copy)
+        nc.scalar.activation(age_cols[0][:], turned[0][:, :, AGE_ROW], ACT.Copy, scale=-1.0)
+        nc.scalar.activation(*lines(0, 0, EARLY_COLS), ACT.Copy)
+        nc.scalar.activation(age_cols[1][:], turned[1][:, :, AGE_ROW], ACT.Copy, scale=-1.0)
+        nc.scalar.activation(*lines(0, EARLY_COLS, NQ), ACT.Copy)
         nc.scalar.activation(*lines(1, 0, SCALAR_COLS), ACT.Copy)
+
+        spread = psum.tile([P, 4, P], F32, name="spread")
+        for c in range(4):
+            nc.tensor.transpose(spread[:, c, :], age_cols[c // 2][:, c % 2 : c % 2 + 1].to_broadcast([P, P]), ident[:])
 
         words = [keep.tile([P, N // 2], U32, name=f"words{h}", align_bytes=256) for h in range(2)]
         for h in range(2):
@@ -134,12 +134,8 @@ def tile_attend_link_age_topk_kernel(tc, qT, k_words, k_scales, ag, rt, offs, ou
         quantize(1)
         part(1, 1, 1, late, 2048)
         part(1, 2, 1, late, 2304)
-        last = late.tile([P, PASSES, 2 * P], U8, name="codes3", offset=2560, align_bytes=256)
-        nc.vector.tensor_copy(
-            last[:].bitcast(U16), words[1][:, P : 2 * P].bitcast(U16).rearrange("p (n o) -> p o n", o=PASSES)
-        )
-        for o in range(PASSES):
-            k_codes[(3, o)] = last[:, o, :]
+        part(0, 3, 1, late, 2560)
+        part(1, 3, 1, late, 2816)
 
         half_decay = keep.tile([P, N], F32, name="half_decay")
         nc.scalar.activation(

from contextlib import ExitStack
import math

import concourse.mybir as mybir
from concourse.masks import make_identity

F32 = mybir.dt.float32
BF16 = mybir.dt.bfloat16
I32 = mybir.dt.int32
U32 = mybir.dt.uint32
U16 = mybir.dt.uint16
U8 = mybir.dt.uint8
FP8X4 = mybir.dt.float8_e4m3fn_x4
FP4X4 = mybir.dt.float4_e2m1fn_x4
ACT = mybir.ActivationFunctionType
ALU = mybir.AluOpType

P = 128
T = 2048
N = 512
NQ = 128
PASSES = 2
PACK = 4
AGE_ROW = 127
AGE_SPLIT = 384
SCALAR_COLS = 80
EARLY_COLS = 48
FLOPS = 2 * 1024 * NQ * N


def tile_attend_link_age_topk_kernel(tc, qT, k_words, k_scales, ag, rt, offs, out):
    nc = tc.nc
    with ExitStack() as ctx:
        keep = ctx.enter_context(tc.tile_pool(name="keep", bufs=1))
        shared = ctx.enter_context(tc.tile_pool(name="shared", bufs=1))
        scaled = ctx.enter_context(tc.tile_pool(name="scaled", bufs=1))
        late = ctx.enter_context(tc.tile_pool(name="late", bufs=1))
        aged = ctx.enter_context(tc.tile_pool(name="aged", bufs=1))
        psum = ctx.enter_context(tc.psum_pool(name="psum", bufs=1))

        scale_pool = scaled.tile([P, T], U8, name="scale_pool", offset=0, align_bytes=512)
        nc.sync.dma_start(scale_pool[32:64, :].bitcast(I32), k_scales.bitcast(I32).rearrange("o f t -> f o t"))
        offsets = keep.tile([P, N // 16], U16, name="offsets")
        nc.sync.dma_start(offsets[:], offs)
        age_pool = keep.tile([P, T], F32, name="age_pool", align_bytes=512)
        nc.scalar.dma_start(age_pool[AGE_ROW:P, :], ag[0:1, :])
        word_pool = shared.tile([P, T], I32, name="word_pool", offset=0, align_bytes=512)
        nc.sync.dma_start(word_pool[:], k_words[0].rearrange("p t b -> p (t b)").bitcast(I32))
        q_raw = [
            late.tile([P, PACK, NQ], F32, name=f"q_raw{o}", offset=2048 * o, align_bytes=512) for o in range(PASSES)
        ]
        q_rows = qT[0].rearrange("(o p j) n -> o p j n", o=PASSES, j=PACK)
        for o in range(PASSES):
            nc.sync.dma_start(q_raw[o][:], q_rows[o])
        rate = keep.tile([P, 1], F32, name="rate", align_bytes=64)
        nc.sync.dma_start(rate[:], rt[0])

        one = keep.tile([P, 1], F32, name="one")
        nc.vector.memset(one[:], 1.0)
        log_half = keep.tile([P, 1], F32, name="log_half")
        nc.scalar.activation(log_half[:], one[:], ACT.Copy, scale=-math.log(2.0))

        scale_above = scale_pool[0:32, :].bitcast(I32)
        scale_below = scale_pool[64:P, :].bitcast(I32)
        age_words = age_pool[0:AGE_ROW, :].bitcast(I32)
        for region, lo, mid, hi in ((scale_above, 0, 255, 512), (scale_below, 0, 255, 512), (age_words, 0, 127, AGE_SPLIT)):
            nc.vector.memset(region[:, lo:mid], 0)
            nc.vector.memset(region[:, mid:hi], 0)
        nc.gpsimd.memset(age_words[:, AGE_SPLIT:T], 0)
        ident = keep.tile([P, P], F32, name="ident")
        make_identity(nc, ident[:])

        scale_rows = keep.tile([P, N], U8, name="scale_rows", align_bytes=512)
        nc.vector.tensor_copy(scale_rows[:], scale_pool[:].indirect(offsets[:]))
        k_planes = scaled.tile([P, PASSES * N], U8, name="k_planes", offset=0, align_bytes=64)
        for quad in range(4):
            nc.sync.dma_start(
                k_planes[32 * quad : 32 * quad + 4, :].bitcast(I32),
                scale_rows[32 + 8 * quad : 32 + 8 * (quad + 1), :].bitcast(I32),
            )

        ages = [aged.tile([P, 2 * P], F32, name=f"ages{h}", offset=1024 * h, align_bytes=256) for h in range(2)]
        nc.scalar.activation(ages[0][:], age_pool[:].indirect(offsets[:, 0:16]), ACT.Copy)
        nc.vector.tensor_copy(ages[1][:, 0:P], age_pool[:].indirect(offsets[:, 16:24]))
        nc.scalar.activation(ages[1][:, P : 2 * P], age_pool[:].indirect(offsets[:, 24:32]), ACT.Copy)
        turned = [psum.tile([P, 2, P], F32, name=f"turned{h}") for h in range(2)]
        for c in range(4):
            nc.tensor.transpose(turned[c // 2][:, c % 2, :], ages[c // 2][:, (c % 2) * P : (c % 2 + 1) * P], ident[:])
        age_cols = [keep.tile([P, 2], F32, name=f"age_cols{h}") for h in range(2)]

        q_bf = [
            aged.tile([P, NQ * PACK], BF16, name=f"q_bf{o}", offset=1024 * o, align_bytes=256) for o in range(PASSES)
        ]

        def lines(o, lo, hi):
            dst = q_bf[o][:, PACK * lo : PACK * hi].rearrange("p (c i j) -> p c j i", i=4, j=PACK)
            return dst, q_raw[o][:, :, lo:hi].rearrange("p j (c i) -> p c j i", i=4)

        nc.scalar.activation(age_cols[0][:], turned[0][:, :, AGE_ROW], ACT.Copy, scale=-1.0)
        nc.scalar.activation(*lines(0, 0, EARLY_COLS), ACT.Copy)
        nc.scalar.activation(age_cols[1][:], turned[1][:, :, AGE_ROW], ACT.Copy, scale=-1.0)
        nc.scalar.activation(*lines(0, EARLY_COLS, NQ), ACT.Copy)
        nc.scalar.activation(*lines(1, 0, SCALAR_COLS), ACT.Copy)

        spread = psum.tile([P, 4, P], F32, name="spread")
        for c in range(4):
            nc.tensor.transpose(spread[:, c, :], age_cols[c // 2][:, c % 2 : c % 2 + 1].to_broadcast([P, P]), ident[:])

        words = [keep.tile([P, N // 2], U32, name=f"words{h}", align_bytes=256) for h in range(2)]
        for h in range(2):
            nc.vector.tensor_copy(words[h][:], word_pool[:].bitcast(U32).indirect(offsets[:, 16 * h : 16 * (h + 1)]))

        q_codes = [shared.tile([P, NQ], U32, name=f"q_codes{o}", offset=512 * o, align_bytes=64) for o in range(PASSES)]
        q_planes = [keep.tile([P, NQ], U8, name=f"q_plane{o}", align_bytes=64) for o in range(PASSES)]
        k_codes = {}

        def quantize(o):
            nc.vector.quantize_mx(
                out=q_codes[o][:].bitcast(FP8X4), scales=q_planes[o][:], in_=q_bf[o][:]
            )

        def part(o, first, count, pool, place):
            codes = pool.tile([P, count * 2 * P], U8, name=f"codes{o}{first}", offset=place, align_bytes=256)
            src = words[first // 2][:, P * (first % 2) : P * (first % 2 + count)]
            nc.vector.tensor_copy(codes[:].bitcast(U16), src.bitcast(U16).rearrange("p (n o) -> p o n", o=PASSES)[:, o, :])
            for i in range(count):
                k_codes[(first + i, o)] = codes[:, 2 * P * i : 2 * P * (i + 1)]

        part(0, 0, 2, late, 4096)
        nc.vector.tensor_copy(*lines(1, SCALAR_COLS, NQ))
        quantize(0)
        part(0, 2, 1, late, 0)
        part(1, 0, 1, late, 256)
        quantize(1)
        part(1, 1, 1, late, 2048)
        part(1, 2, 1, late, 2304)
        part(0, 3, 1, late, 2560)
        part(1, 3, 1, late, 2816)

        half_decay = keep.tile([P, N], F32, name="half_decay")
        nc.scalar.activation(
            half_decay[:], spread[:].rearrange("p c n -> p (c n)"), ACT.Exp, scale=rate[:, 0:1], bias=log_half[:, 0:1]
        )

        scores = [psum.tile([P, P], F32, name=f"scores{c}") for c in range(4)]
        for c, o in [(c, o) for o in range(PASSES) for c in range(3)] + [(3, o) for o in range(PASSES)]:
            nc.tensor.matmul_mx(
                out=scores[c][:],
                lhsT=q_codes[o][:].bitcast(FP8X4),
                lhsT_scale=q_planes[o][:],
                rhs=k_codes[(c, o)].bitcast(FP4X4),
                rhs_scale=k_planes[:, o * N + P * c : o * N + P * (c + 1)],
                start=(o == 0),
                stop=(o == PASSES - 1),
            )

        res = [keep.tile([P, 2, P], F32, name=f"res{h}", align_bytes=512) for h in range(2)]
        pieces = [(0, P), (P, 2 * P), (2 * P, 3 * P), (3 * P, 3 * P + P // 2), (3 * P + P // 2, N)]
        for lo, hi in pieces:
            c = lo // P
            th = keep.tile([P, hi - lo], F32, name=f"th{lo}")
            nc.scalar.activation(th[:], scores[c][:, lo - c * P : hi - c * P], ACT.Tanh, scale=0.5)
            half = lo // (2 * P)
            flat = res[half][:].rearrange("p a n -> p (a n)")
            nc.vector.scalar_tensor_tensor(
                flat[:, lo - half * 2 * P : hi - half * 2 * P], th[:], 1.0, half_decay[:, lo:hi], ALU.add, ALU.mult
            )
            if hi % (2 * P) == 0:
                nc.sync.dma_start(out[0, :, hi - 2 * P : hi], flat)
